import numpy as np
import ml_dtypes


def mxq(x, axis, fmt="e4m3"):
    dtype, down = {"e4m3": (ml_dtypes.float8_e4m3fn, 7), "e5m2": (ml_dtypes.float8_e5m2, 14)}[fmt]
    v = np.moveaxis(np.asarray(x, np.float32).astype(ml_dtypes.bfloat16).astype(np.float64), axis, -1)
    blocks = v.reshape(v.shape[:-1] + (-1, 32))
    amax = np.abs(blocks).max(-1, keepdims=True)
    byte = np.maximum(np.where(amax > 0, np.frexp(amax)[1] - 1 + 127, 0) - down, 1)
    scale = np.exp2(byte - 127.0)
    codes = (blocks / scale).astype(np.float32).astype(dtype).astype(np.float64)
    return np.moveaxis((codes * scale).reshape(v.shape), -1, axis)


WIDE = False


def mx_kscale(k):
    if not WIDE:
        return np.ones(k)
    levels = np.array([10, -10, 5, -5, 0])
    if k % 512:
        return np.exp2(np.random.permutation(np.resize(levels, k // 32))).repeat(32)
    a = np.empty((k // 512, 16))
    for p in range(k // 512):
        a[p, :8] = np.random.permutation(np.resize(levels, 8))
        for g in range(8):
            far = levels[np.abs(levels - a[p, g]) >= 10]
            a[p, g + 8] = far[np.random.randint(len(far))]
    return np.exp2(a.ravel()).repeat(32)


def f64(x):
    return np.asarray(x).astype(np.float64)


def striped(idx):
    return np.tile(idx.reshape(-1, 16).T, (8, 1)).astype(np.uint16)


def unstriped(offs):
    return offs[:16].T.reshape(-1).astype(np.int64)


E2M1 = np.array([0.0, 0.5, 1.0, 1.5, 2.0, 3.0, 4.0, 6.0, -0.0, -0.5, -1.0, -1.5, -2.0, -3.0, -4.0, -6.0])


def pack_weight(w, fmt):
    k, n = w.shape
    w = f64(np.asarray(w, np.float32).astype(ml_dtypes.bfloat16)).reshape(k // 32, 32, n)
    amax = np.abs(w).max(1)
    if fmt == "e4m3":
        byte = np.frexp(amax)[1] - 1 + 127 - 7
    else:
        mant, ex = np.frexp(amax / 6.0)
        byte = np.where(mant > 0.5, ex, ex - 1) + 127
    byte = np.clip(np.where(amax > 0, byte, 1), 1, 254)
    scaled = (w * np.exp2(127.0 - byte)[:, None, :]).reshape(k, n).astype(np.float32)
    by_word = np.ascontiguousarray(scaled.reshape(k // 512, 128, 4, n).transpose(0, 1, 3, 2))
    if fmt == "e4m3":
        words = by_word.astype(ml_dtypes.float8_e4m3fn).view(np.uint8)
    else:
        c = by_word.astype(ml_dtypes.float4_e2m1fn).view(np.uint8) & 0xF
        words = (c[..., 0::2] | (c[..., 1::2] << 4)).reshape(k // 512, 128, 2 * n)
    return np.ascontiguousarray(words), np.ascontiguousarray(byte.astype(np.uint8).reshape(k // 512, 16, n))


def unpack_weight(words, scales, fmt):
    g, _, n = scales.shape
    words = np.ascontiguousarray(words).reshape(g, 128, n, -1)
    if fmt == "e4m3":
        vals = words.view(ml_dtypes.float8_e4m3fn).astype(np.float64)
    else:
        nib = np.empty((g, 128, n, 4), np.uint8)
        nib[..., 0::2] = words & 0xF
        nib[..., 1::2] = words >> 4
        vals = E2M1[nib]
    vals = vals * np.repeat(np.exp2(scales.astype(np.float64) - 127.0), 8, axis=1)[..., None]
    return vals.transpose(0, 1, 3, 2).reshape(g * 512, n)


def gelu(v):
    return 0.5 * v * (1.0 + np.tanh(np.sqrt(2.0 / np.pi) * (v + 0.044715 * v**3)))


K, T, S, H, N = 1536, 2048, 1024, 512, 384

def setup_inputs():
    n = np.random.standard_normal
    s = mx_kscale(K)[:, None]
    u = mx_kscale(H)[:, None]
    tab_words, tab_scales = pack_weight(n((K, T)) * s, "e4m3")
    we = (n((K, H)) / np.sqrt(K) / s * u.T).astype(np.float32)
    wi_words, wi_scales = pack_weight(n((K, H)) / np.sqrt(K) / s * u.T, "e2m1")
    gT = np.exp(0.3 * n((H, T))).astype(np.float32)
    wo = (n((H, N)) / np.sqrt(H) / u).astype(np.float32)
    bo = (0.3 * n(N)).astype(np.float32)
    offs = striped(np.random.permutation(T)[:S])
    return dict(tab_words=tab_words, tab_scales=tab_scales, offs=offs, we=we,
                wi_words=wi_words, wi_scales=wi_scales, gT=gT, wo=wo, bo=bo)

def reference(tab_words, tab_scales, offs, we, wi_words, wi_scales, gT, wo, bo):
    v = unpack_weight(tab_words, tab_scales, "e4m3")[:, unstriped(offs)]
    g = f64(gT)[:, unstriped(offs)]
    wi = unpack_weight(wi_words, wi_scales, "e2m1")
    e = mxq(f64(we), 0, "e4m3").T @ v
    i = wi.T @ v
    h = (np.maximum(e, 0.0) - np.maximum(i, 0.0)) * g
    y = mxq(f64(wo), 0, "e4m3").T @ mxq(h, 0, "e4m3")
    return y + f64(bo)[:, None]

@@ -1,0 +1,273 @@
+from contextlib import ExitStack
+
+import concourse.mybir as mybir
+
+K, T, S, H, N = 1536, 2048, 1024, 512, 384
+FLOPS = 2 * S * (2 * K * H + H * N)
+
+F32 = mybir.dt.float32
+BF16 = mybir.dt.bfloat16
+I32 = mybir.dt.int32
+U32 = mybir.dt.uint32
+U16 = mybir.dt.uint16
+U8 = mybir.dt.uint8
+FP8X4 = mybir.dt.float8_e4m3fn_x4
+FP4X4 = mybir.dt.float4_e2m1fn_x4
+ALU = mybir.AluOpType
+ACT = mybir.ActivationFunctionType
+
+P = 128
+PASSES = K // 512
+SLOTS = 4
+HALF = 512
+OUT_TILES = N // P
+CHUNKS = [(0, 256, "s", "s"), (256, 256, "s", "s"), (512, 256, "s", "s"), (768, 128, "v", "v"), (896, 128, "v", "v")]
+
+
+def tile_list_net_drive_trials_kernel(tc, tab_words, tab_scales, offs, we, wi_words, wi_scales, gT, wo, bo, out):
+    nc = tc.nc
+    with ExitStack() as ctx:
+        keep = ctx.enter_context(tc.tile_pool(name="keep", bufs=1))
+        psum = ctx.enter_context(tc.psum_pool(name="psum", bufs=1))
+
+        offsets = keep.tile([P, S // 16], U16, name="offsets")
+        tab = [keep.tile([P, T], I32, name=f"tab{a}") for a in range(PASSES)]
+        tab_sc = keep.tile([P, T // 4], I32, name="tab_sc")
+        v_words = [keep.tile([P, S], U32, name=f"v_words{a}", align_bytes=64) for a in range(PASSES)]
+        v_sc = keep.tile([P, S], U8, name="v_sc", align_bytes=64)
+        v_sc_low = keep.tile([P, PASSES - 1, S], U8, name="v_sc_low", align_bytes=64)
+        we_raw = [keep.tile([P, SLOTS, H], F32, name=f"we_raw{a}") for a in range(PASSES)]
+        we_bf = [keep.tile([P, SLOTS * H], BF16, name=f"we_bf{a}", align_bytes=64) for a in range(PASSES)]
+        we_codes = [keep.tile([P, H], U32, name=f"we_codes{a}", align_bytes=64) for a in range(PASSES)]
+        we_sc = [keep.tile([P, H], U8, name=f"we_sc{a}", align_bytes=64) for a in range(PASSES)]
+        wi_raw = keep.tile([P, PASSES, 2 * H // 4], I32, name="wi_raw")
+        wi_sc_raw = keep.tile([P, PASSES, H // 4], I32, name="wi_sc_raw")
+        wi_codes = keep.tile([P, SLOTS, PASSES, 2 * P], U8, name="wi_codes", align_bytes=64)
+        wi_sc = keep.tile([P, SLOTS, PASSES, P], U8, name="wi_sc", align_bytes=64)
+        gain = [keep.tile([P, T], F32, name=f"gain{t}") for t in range(SLOTS)]
+        wo_raw = keep.tile([P, SLOTS, N], F32, name="wo_raw")
+        wo_bf = keep.tile([P, SLOTS * N], BF16, name="wo_bf", align_bytes=64)
+        wo_codes = keep.tile([P, N], U32, name="wo_codes", align_bytes=64)
+        wo_sc = keep.tile([P, N], U8, name="wo_sc", align_bytes=64)
+        bias = keep.tile([P, OUT_TILES], F32, name="bias")
+        relu_i = keep.tile([P, SLOTS, S], F32, name="relu_i")
+        diff = keep.tile([P, SLOTS, S], F32, name="diff")
+        h_f32 = keep.tile([P, SLOTS, S], F32, name="h_f32")
+        h_bf = keep.tile([P, SLOTS * S], BF16, name="h_bf", align_bytes=64)
+        h_codes = keep.tile([P, S], U32, name="h_codes", align_bytes=64)
+        h_sc = keep.tile([P, S], U8, name="h_sc", align_bytes=64)
+        result = keep.tile([P, OUT_TILES, S], F32, name="result")
+        i_bank = [psum.tile([P, HALF], F32, name=f"i_bank{t}") for t in range(SLOTS)]
+        e_bank = [psum.tile([P, HALF], F32, name=f"e_bank{t}") for t in range(SLOTS)]
+
+        def picks(first, width):
+            return offsets[:, first // 16 : (first + width) // 16]
+
+        nc.vector.memset(tab_sc[:], 0)
+        nc.vector.memset(wi_sc_raw[:], 0)
+        nc.vector.memset(v_sc_low[:].rearrange("p a s -> p (a s)").bitcast(I32), 0)
+
+        nc.sync.dma_start(offsets[:], offs)
+        for q in range(4):
+            nc.gpsimd.dma_start(
+                tab_sc[32 * q : 32 * q + 4 * PASSES, :], tab_scales[:, 4 * q : 4 * q + 4, :].bitcast(I32)
+            )
+        for q in range(4):
+            nc.gpsimd.dma_start(
+                wi_sc_raw[32 * q : 32 * q + 4, :, :],
+                wi_scales[:, 4 * q : 4 * q + 4, :].bitcast(I32).rearrange("a r c -> r a c"),
+            )
+        with nc.allow_non_contiguous_dma(reason="one bias value for each partition and output tile"):
+            nc.gpsimd.dma_start(bias[:], bo.rearrange("(c p) -> p c", p=P))
+
+        def load_tab(a):
+            nc.sync.dma_start(tab[a][:], tab_words[a].rearrange("p t i -> p (t i)").bitcast(I32))
+
+        def load_we(a):
+            nc.sync.dma_start(we_raw[a][:], we[512 * a : 512 * (a + 1), :].rearrange("(p j) r -> p j r", j=4))
+
+        gain_rows = gT.rearrange("(w t b) c -> t w b c", t=SLOTS, b=4)
+        wo_rows = wo.rearrange("(w t b) n -> t w b n", t=SLOTS, b=4)
+        load_tab(0)
+        load_we(0)
+        load_tab(1)
+        nc.sync.dma_start(wi_raw[:], wi_words.bitcast(I32).rearrange("a p c -> p a c"))
+        load_we(1)
+        load_tab(2)
+        load_we(2)
+        nc.sync.dma_start(gain[0][:], gain_rows[0])
+        nc.sync.dma_start(gain[1][:], gain_rows[1])
+        for t in range(SLOTS):
+            nc.sync.dma_start(wo_raw[:, t, :], wo_rows[t])
+        nc.sync.dma_start(gain[2][:], gain_rows[2])
+        nc.sync.dma_start(gain[3][:], gain_rows[3])
+
+        def gather_words(a, first, width):
+            nc.vector.tensor_copy(
+                v_words[a][:, first : first + width], tab[a][:].bitcast(U32).indirect(picks(first, width))
+            )
+
+        def round_we(a, t):
+            nc.scalar.activation(
+                we_bf[a][:, H * t : H * (t + 1)].rearrange("p (w b j) -> p w j b", b=4, j=4),
+                we_raw[a][:].rearrange("p j (w t b) -> p t w j b", t=SLOTS, b=4)[:, t],
+                ACT.Copy,
+            )
+
+        def quantize_we(a, first, width):
+            nc.vector.quantize_mx(
+                out=we_codes[a][:, first : first + width].bitcast(FP8X4),
+                scales=we_sc[a][:, first : first + width],
+                in_=we_bf[a][:, 4 * first : 4 * (first + width)],
+            )
+
+        def excite(t, half, a):
+            cols = slice(HALF * half, HALF * (half + 1))
+            nc.tensor.matmul_mx(
+                out=e_bank[t][:],
+                lhsT=we_codes[a][:, P * t : P * (t + 1)].bitcast(FP8X4),
+                lhsT_scale=we_sc[a][:, P * t : P * (t + 1)],
+                rhs=v_words[a][:, cols].bitcast(FP8X4),
+                rhs_scale=v_sc[4 * a :, cols],
+                start=(a == 0),
+                stop=(a == PASSES - 1),
+            )
+
+        def inhibit(t, half, a):
+            cols = slice(HALF * half, HALF * (half + 1))
+            nc.tensor.matmul_mx(
+                out=i_bank[t][:],
+                lhsT=wi_codes[:, t, a, :].bitcast(FP4X4),
+                lhsT_scale=wi_sc[:, t, a, :],
+                rhs=v_words[a][:, cols].bitcast(FP8X4),
+                rhs_scale=v_sc[:, cols] if a == 0 else v_sc_low[:, a - 1, cols],
+                start=(a == 0),
+                stop=(a == PASSES - 1),
+            )
+
+        gather_words(0, 0, S)
+        nc.vector.tensor_copy(v_sc[:], tab_sc[:].bitcast(U8).indirect(picks(0, S)))
+        for a in range(1, PASSES):
+            nc.gpsimd.dma_start(
+                v_sc_low[0:112, a - 1, :].bitcast(I32), v_sc[4 * a : 4 * a + 112, :].bitcast(I32)
+            )
+        for t in range(SLOTS):
+            round_we(0, t)
+        quantize_we(0, 0, H)
+        for t in range(SLOTS):
+            excite(t, 0, 0)
+        gather_words(1, 0, S)
+        nc.vector.tensor_copy(
+            wi_codes[:].rearrange("p t a c -> p t (a c)").bitcast(I32).rearrange("p t (u e) -> p t u e", e=2),
+            wi_raw[:].rearrange("p a (w t e) -> p t (a w) e", t=SLOTS, e=2),
+        )
+        nc.vector.tensor_copy(
+            wi_sc[:].rearrange("p t a c -> p t (a c)").bitcast(I32),
+            wi_sc_raw[:].rearrange("p a (w t) -> p t (a w)", t=SLOTS),
+        )
+        for a in range(2):
+            for t in range(SLOTS):
+                inhibit(t, 0, a)
+        for t in range(SLOTS):
+            round_we(1, t)
+        quantize_we(1, 0, H)
+        for t in range(SLOTS):
+            excite(t, 0, 1)
+        gather_words(2, 0, HALF)
+
+        def rectify_i(t, half):
+            nc.scalar.activation(relu_i[:, t, HALF * half : HALF * (half + 1)], i_bank[t][:], ACT.Relu)
+
+        def subtract(t, half):
+            cols = slice(HALF * half, HALF * (half + 1))
+            nc.vector.scalar_tensor_tensor(
+                diff[:, t, cols], e_bank[t][:], 0.0, relu_i[:, t, cols], ALU.max, ALU.subtract
+            )
+
+        def apply_gain(t, first, width):
+            cols = slice(first, first + width)
+            nc.vector.tensor_tensor(
+                h_f32[:, t, cols], gain[t][:].indirect(picks(first, width)), diff[:, t, cols], ALU.mult
+            )
+
+        out_rows = out.rearrange("(c p) j -> p c j", p=P)
+
+        def finish(first, width, round_on, empty_on, banks):
+            cols = slice(first, first + width)
+            h_dst = h_bf[:, 4 * first : 4 * (first + width)].rearrange("p (c i t) -> p c t i", i=4, t=SLOTS)
+            h_src = h_f32[:, :, cols].rearrange("p t (c i) -> p c t i", i=4)
+            if round_on == "s":
+                nc.scalar.activation(h_dst, h_src, ACT.Copy)
+            else:
+                nc.vector.tensor_copy(h_dst, h_src)
+            nc.vector.quantize_mx(
+                out=h_codes[:, cols].bitcast(FP8X4),
+                scales=h_sc[:, cols],
+                in_=h_bf[:, 4 * first : 4 * (first + width)],
+            )
+            per_bank = HALF // width
+            sums = [
+                banks[c // per_bank][:, width * (c % per_bank) : width * (c % per_bank + 1)] for c in range(OUT_TILES)
+            ]
+            for c in range(OUT_TILES):
+                nc.tensor.matmul_mx(
+                    out=sums[c],
+                    lhsT=wo_codes[:, P * c : P * (c + 1)].bitcast(FP8X4),
+                    lhsT_scale=wo_sc[:, P * c : P * (c + 1)],
+                    rhs=h_codes[:, cols].bitcast(FP8X4),
+                    rhs_scale=h_sc[:, cols],
+                    start=True,
+                    stop=True,
+                )
+            for c in range(OUT_TILES):
+                if empty_on == "s":
+                    nc.scalar.activation(result[:, c, cols], sums[c], ACT.Identity, bias=bias[:, c : c + 1])
+                else:
+                    nc.vector.tensor_scalar(result[:, c, cols], sums[c], bias[:, c : c + 1], None, ALU.add)
+            nc.sync.dma_start(out_rows[:, :, cols], result[:, :, cols])
+
+        for t in range(SLOTS):
+            inhibit(t, 0, 2)
+            rectify_i(t, 0)
+            round_we(2, t)
+            quantize_we(2, P * t, P)
+            excite(t, 0, 2)
+            subtract(t, 0)
+            if t == 0:
+                gather_words(2, HALF, HALF)
+            if t < SLOTS - 1:
+                apply_gain(t, 0, HALF)
+
+        for t in range(SLOTS):
+            for a in range(PASSES):
+                inhibit(t, 1, a)
+            rectify_i(t, 1)
+            for a in range(PASSES):
+                excite(t, 1, a)
+
+        nc.scalar.activation(
+            wo_bf[:].rearrange("p (c i t) -> p c t i", i=4, t=SLOTS),
+            wo_raw[:].rearrange("p t (c i) -> p c t i", i=4),
+            ACT.Copy,
+        )
+        for first, width in ((0, 256), (256, 128)):
+            nc.vector.quantize_mx(
+                out=wo_codes[:, first : first + width].bitcast(FP8X4),
+                scales=wo_sc[:, first : first + width],
+                in_=wo_bf[:, 4 * first : 4 * (first + width)],
+            )
+
+        chunk_banks = [i_bank[0:2], i_bank[2:4], i_bank[0:2], e_bank[0:1], e_bank[1:2]]
+        for k in range(2):
+            apply_gain(3, CHUNKS[k][0], CHUNKS[k][1])
+        for k in range(2):
+            finish(*CHUNKS[k], chunk_banks[k])
+        for t in range(SLOTS):
+            subtract(t, 1)
+            if t < 2:
+                apply_gain(t, HALF, HALF)
+        for k in range(2, len(CHUNKS)):
+            for t in range(2, SLOTS):
+                apply_gain(t, CHUNKS[k][0], CHUNKS[k][1])
+        for k in range(2, len(CHUNKS)):
+            finish(*CHUNKS[k], chunk_banks[k])

@@ -21,7 +21,7 @@ PASSES = K // 512
 SLOTS = 4
 HALF = 512
 OUT_TILES = N // P
-CHUNKS = [(0, 256, "s", "s"), (256, 256, "s", "s"), (512, 256, "s", "s"), (768, 128, "v", "v"), (896, 128, "v", "v")]
+CHUNKS = [(0, 256, "s", "sss"), (256, 256, "s", "sss"), (512, 256, "s", "sss"), (768, 128, "s", "sss"), (896, 128, "v", "vvs")]
 
 
 def tile_list_net_drive_trials_kernel(tc, tab_words, tab_scales, offs, we, wi_words, wi_scales, gT, wo, bo, out):
@@ -30,77 +30,51 @@ def tile_list_net_drive_trials_kernel(tc, tab_words, tab_scales, offs, we, wi_wo
         keep = ctx.enter_context(tc.tile_pool(name="keep", bufs=1))
         psum = ctx.enter_context(tc.psum_pool(name="psum", bufs=1))
 
+        def sbuf(name, shape, dtype, slot=None):
+            return keep.tile(shape, dtype, name=name, tag=slot or name, align_bytes=64)
+
         offsets = keep.tile([P, S // 16], U16, name="offsets")
-        tab = [keep.tile([P, T], I32, name=f"tab{a}") for a in range(PASSES)]
-        tab_sc = keep.tile([P, T // 4], I32, name="tab_sc")
-        v_words = [keep.tile([P, S], U32, name=f"v_words{a}", align_bytes=64) for a in range(PASSES)]
-        v_sc = keep.tile([P, S], U8, name="v_sc", align_bytes=64)
-        v_sc_low = keep.tile([P, PASSES - 1, S], U8, name="v_sc_low", align_bytes=64)
-        we_raw = [keep.tile([P, SLOTS, H], F32, name=f"we_raw{a}") for a in range(PASSES)]
-        we_bf = [keep.tile([P, SLOTS * H], BF16, name=f"we_bf{a}", align_bytes=64) for a in range(PASSES)]
-        we_codes = [keep.tile([P, H], U32, name=f"we_codes{a}", align_bytes=64) for a in range(PASSES)]
-        we_sc = [keep.tile([P, H], U8, name=f"we_sc{a}", align_bytes=64) for a in range(PASSES)]
-        wi_raw = keep.tile([P, PASSES, 2 * H // 4], I32, name="wi_raw")
-        wi_sc_raw = keep.tile([P, PASSES, H // 4], I32, name="wi_sc_raw")
-        wi_codes = keep.tile([P, SLOTS, PASSES, 2 * P], U8, name="wi_codes", align_bytes=64)
-        wi_sc = keep.tile([P, SLOTS, PASSES, P], U8, name="wi_sc", align_bytes=64)
-        gain = [keep.tile([P, T], F32, name=f"gain{t}") for t in range(SLOTS)]
-        wo_raw = keep.tile([P, SLOTS, N], F32, name="wo_raw")
-        wo_bf = keep.tile([P, SLOTS * N], BF16, name="wo_bf", align_bytes=64)
-        wo_codes = keep.tile([P, N], U32, name="wo_codes", align_bytes=64)
-        wo_sc = keep.tile([P, N], U8, name="wo_sc", align_bytes=64)
-        bias = keep.tile([P, OUT_TILES], F32, name="bias")
-        relu_i = keep.tile([P, SLOTS, S], F32, name="relu_i")
-        diff = keep.tile([P, SLOTS, S], F32, name="diff")
-        h_f32 = keep.tile([P, SLOTS, S], F32, name="h_f32")
-        h_bf = keep.tile([P, SLOTS * S], BF16, name="h_bf", align_bytes=64)
-        h_codes = keep.tile([P, S], U32, name="h_codes", align_bytes=64)
-        h_sc = keep.tile([P, S], U8, name="h_sc", align_bytes=64)
-        result = keep.tile([P, OUT_TILES, S], F32, name="result")
+        tab_sc = sbuf("tab_sc", [P, T // 4], I32, "slot_a")
+        v_words = [sbuf(f"v_words{a}", [P, S], U32) for a in range(PASSES)]
+        v_sc = sbuf("v_sc", [P, S], U8)
+        v_sc_low = sbuf("v_sc_low", [P, PASSES - 1, S], U8)
+        we_codes = [sbuf(f"we_codes{a}", [P, H], U32) for a in range(PASSES)]
+        we_sc = [sbuf(f"we_sc{a}", [P, H], U8) for a in range(PASSES)]
+        wi_raw = sbuf("wi_raw", [P, PASSES, 2 * H // 4], I32)
+        wi_sc_raw = sbuf("wi_sc_raw", [P, PASSES, H // 4], I32)
+        wi_codes = sbuf("wi_codes", [P, SLOTS, PASSES, 2 * P], U8)
+        wi_sc = sbuf("wi_sc", [P, SLOTS, PASSES, P], U8)
+        wo_bf = sbuf("wo_bf", [P, SLOTS * N], BF16)
+        wo_codes = sbuf("wo_codes", [P, N], U32)
+        wo_sc = sbuf("wo_sc", [P, N], U8)
+        bias = sbuf("bias", [P, OUT_TILES], F32)
+        relu_i = sbuf("relu_i", [P, SLOTS, S], F32)
+        h_bf = sbuf("h_bf", [P, SLOTS * S], BF16)
+        h_codes = sbuf("h_codes", [P, S], U32)
+        h_sc = sbuf("h_sc", [P, S], U8)
+        result = sbuf("result", [P, OUT_TILES, S], F32)
         i_bank = [psum.tile([P, HALF], F32, name=f"i_bank{t}") for t in range(SLOTS)]
         e_bank = [psum.tile([P, HALF], F32, name=f"e_bank{t}") for t in range(SLOTS)]
+        tab, we_raw, we_bf, gain = {}, {}, {}, {}
+
+        gain_rows = gT.rearrange("(w t b) c -> t w b c", t=SLOTS, b=4)
+        wo_rows = wo.rearrange("(w t b) n -> t w b n", t=SLOTS, b=4)
+        out_rows = out.rearrange("(c p) j -> p c j", p=P)
 
         def picks(first, width):
             return offsets[:, first // 16 : (first + width) // 16]
 
-        nc.vector.memset(tab_sc[:], 0)
-        nc.vector.memset(wi_sc_raw[:], 0)
-        nc.vector.memset(v_sc_low[:].rearrange("p a s -> p (a s)").bitcast(I32), 0)
-
-        nc.sync.dma_start(offsets[:], offs)
-        for q in range(4):
-            nc.gpsimd.dma_start(
-                tab_sc[32 * q : 32 * q + 4 * PASSES, :], tab_scales[:, 4 * q : 4 * q + 4, :].bitcast(I32)
-            )
-        for q in range(4):
-            nc.gpsimd.dma_start(
-                wi_sc_raw[32 * q : 32 * q + 4, :, :],
-                wi_scales[:, 4 * q : 4 * q + 4, :].bitcast(I32).rearrange("a r c -> r a c"),
-            )
-        with nc.allow_non_contiguous_dma(reason="one bias value for each partition and output tile"):
-            nc.gpsimd.dma_start(bias[:], bo.rearrange("(c p) -> p c", p=P))
-
-        def load_tab(a):
+        def load_tab(a, slot):
+            tab[a] = sbuf(f"tab{a}", [P, T], I32, slot)
             nc.sync.dma_start(tab[a][:], tab_words[a].rearrange("p t i -> p (t i)").bitcast(I32))
 
-        def load_we(a):
+        def load_we(a, slot):
+            we_raw[a] = sbuf(f"we_raw{a}", [P, SLOTS, H], F32, slot)
             nc.sync.dma_start(we_raw[a][:], we[512 * a : 512 * (a + 1), :].rearrange("(p j) r -> p j r", j=4))
 
-        gain_rows = gT.rearrange("(w t b) c -> t w b c", t=SLOTS, b=4)
-        wo_rows = wo.rearrange("(w t b) n -> t w b n", t=SLOTS, b=4)
-        load_tab(0)
-        load_we(0)
-        load_tab(1)
-        nc.sync.dma_start(wi_raw[:], wi_words.bitcast(I32).rearrange("a p c -> p a c"))
-        load_we(1)
-        load_tab(2)
-        load_we(2)
-        nc.sync.dma_start(gain[0][:], gain_rows[0])
-        nc.sync.dma_start(gain[1][:], gain_rows[1])
-        for t in range(SLOTS):
-            nc.sync.dma_start(wo_raw[:, t, :], wo_rows[t])
-        nc.sync.dma_start(gain[2][:], gain_rows[2])
-        nc.sync.dma_start(gain[3][:], gain_rows[3])
+        def load_gain(t, slot):
+            gain[t] = sbuf(f"gain{t}", [P, T], F32, slot)
+            nc.sync.dma_start(gain[t][:], gain_rows[t])
 
         def gather_words(a, first, width):
             nc.vector.tensor_copy(
@@ -145,57 +119,26 @@ def tile_list_net_drive_trials_kernel(tc, tab_words, tab_scales, offs, we, wi_wo
                 stop=(a == PASSES - 1),
             )
 
-        gather_words(0, 0, S)
-        nc.vector.tensor_copy(v_sc[:], tab_sc[:].bitcast(U8).indirect(picks(0, S)))
-        for a in range(1, PASSES):
-            nc.gpsimd.dma_start(
-                v_sc_low[0:112, a - 1, :].bitcast(I32), v_sc[4 * a : 4 * a + 112, :].bitcast(I32)
-            )
-        for t in range(SLOTS):
-            round_we(0, t)
-        quantize_we(0, 0, H)
-        for t in range(SLOTS):
-            excite(t, 0, 0)
-        gather_words(1, 0, S)
-        nc.vector.tensor_copy(
-            wi_codes[:].rearrange("p t a c -> p t (a c)").bitcast(I32).rearrange("p t (u e) -> p t u e", e=2),
-            wi_raw[:].rearrange("p a (w t e) -> p t (a w) e", t=SLOTS, e=2),
-        )
-        nc.vector.tensor_copy(
-            wi_sc[:].rearrange("p t a c -> p t (a c)").bitcast(I32),
-            wi_sc_raw[:].rearrange("p a (w t) -> p t (a w)", t=SLOTS),
-        )
-        for a in range(2):
-            for t in range(SLOTS):
-                inhibit(t, 0, a)
-        for t in range(SLOTS):
-            round_we(1, t)
-        quantize_we(1, 0, H)
-        for t in range(SLOTS):
-            excite(t, 0, 1)
-        gather_words(2, 0, HALF)
-
         def rectify_i(t, half):
             nc.scalar.activation(relu_i[:, t, HALF * half : HALF * (half + 1)], i_bank[t][:], ACT.Relu)
 
-        def subtract(t, half):
-            cols = slice(HALF * half, HALF * (half + 1))
+        def subtract(t, first, width, dst):
             nc.vector.scalar_tensor_tensor(
-                diff[:, t, cols], e_bank[t][:], 0.0, relu_i[:, t, cols], ALU.max, ALU.subtract
+                dst,
+                e_bank[t][:, first % HALF : first % HALF + width],
+                0.0,
+                relu_i[:, t, first : first + width],
+                ALU.max,
+                ALU.subtract,
             )
 
-        def apply_gain(t, first, width):
-            cols = slice(first, first + width)
-            nc.vector.tensor_tensor(
-                h_f32[:, t, cols], gain[t][:].indirect(picks(first, width)), diff[:, t, cols], ALU.mult
-            )
+        def apply_gain(t, first, width, dst, src):
+            nc.vector.tensor_tensor(dst, gain[t][:].indirect(picks(first, width)), src, ALU.mult)
 
-        out_rows = out.rearrange("(c p) j -> p c j", p=P)
-
-        def finish(first, width, round_on, empty_on, banks):
+        def finish(first, width, round_on, empty_on, h_f32, banks):
             cols = slice(first, first + width)
             h_dst = h_bf[:, 4 * first : 4 * (first + width)].rearrange("p (c i t) -> p c t i", i=4, t=SLOTS)
-            h_src = h_f32[:, :, cols].rearrange("p t (c i) -> p c t i", i=4)
+            h_src = h_f32.rearrange("p t (c i) -> p c t i", i=4)
             if round_on == "s":
                 nc.scalar.activation(h_dst, h_src, ACT.Copy)
             else:
@@ -205,7 +148,7 @@ def tile_list_net_drive_trials_kernel(tc, tab_words, tab_scales, offs, we, wi_wo
                 scales=h_sc[:, cols],
                 in_=h_bf[:, 4 * first : 4 * (first + width)],
             )
-            per_bank = HALF // width
+            per_bank = -(-OUT_TILES // len(banks))
             sums = [
                 banks[c // per_bank][:, width * (c % per_bank) : width * (c % per_bank + 1)] for c in range(OUT_TILES)
             ]
@@ -220,23 +163,96 @@ def tile_list_net_drive_trials_kernel(tc, tab_words, tab_scales, offs, we, wi_wo
                     stop=True,
                 )
             for c in range(OUT_TILES):
-                if empty_on == "s":
+                if empty_on[c] == "s":
                     nc.scalar.activation(result[:, c, cols], sums[c], ACT.Identity, bias=bias[:, c : c + 1])
                 else:
                     nc.vector.tensor_scalar(result[:, c, cols], sums[c], bias[:, c : c + 1], None, ALU.add)
             nc.sync.dma_start(out_rows[:, :, cols], result[:, :, cols])
 
+        nc.vector.memset(tab_sc[:], 0)
+        nc.vector.memset(wi_sc_raw[:], 0)
+        nc.vector.memset(v_sc_low[:].rearrange("p a s -> p (a s)").bitcast(I32), 0)
+        nc.sync.dma_start(offsets[:], offs)
+        load_tab(0, "tab0")
+        load_we(0, "we_raw0")
+        for q in range(4):
+            nc.sync.dma_start(
+                tab_sc[32 * q : 32 * q + 4 * PASSES, :], tab_scales[:, 4 * q : 4 * q + 4, :].bitcast(I32)
+            )
+        load_tab(1, "slot_c")
+        for q in range(4):
+            nc.sync.dma_start(
+                wi_sc_raw[32 * q : 32 * q + 4, :, :],
+                wi_scales[:, 4 * q : 4 * q + 4, :].bitcast(I32).rearrange("a r c -> r a c"),
+            )
+        nc.sync.dma_start(wi_raw[:], wi_words.bitcast(I32).rearrange("a p c -> p a c"))
+        load_we(1, "slot_d")
+        with nc.allow_non_contiguous_dma(reason="one bias value for each partition and output tile"):
+            nc.sync.dma_start(bias[:], bo.rearrange("(c p) -> p c", p=P))
+
+        gather_words(0, 0, S)
+        nc.vector.tensor_copy(v_sc[:], tab_sc[:].bitcast(U8).indirect(picks(0, S)))
+        for a in range(1, PASSES):
+            nc.sync.dma_start(
+                v_sc_low[0:112, a - 1, :].bitcast(I32), v_sc[4 * a : 4 * a + 112, :].bitcast(I32)
+            )
+        load_tab(2, "slot_a")
+        we_bf[0] = sbuf("we_bf0", [P, SLOTS * H], BF16, "slot_b")
+        for t in range(SLOTS):
+            round_we(0, t)
+        quantize_we(0, 0, H)
+        load_we(2, "slot_b")
+        for t in range(SLOTS):
+            excite(t, 0, 0)
+
+        gather_words(1, 0, S)
+        load_gain(0, "slot_c")
+        nc.vector.tensor_copy(
+            wi_codes[:].rearrange("p t a c -> p t (a c)").bitcast(I32).rearrange("p t (u e) -> p t u e", e=2),
+            wi_raw[:].rearrange("p a (w t e) -> p t (a w) e", t=SLOTS, e=2),
+        )
+        nc.vector.tensor_copy(
+            wi_sc[:].rearrange("p t a c -> p t (a c)").bitcast(I32),
+            wi_sc_raw[:].rearrange("p a (w t) -> p t (a w)", t=SLOTS),
+        )
+        for a in range(2):
+            for t in range(SLOTS):
+                inhibit(t, 0, a)
+        we_bf[1] = sbuf("we_bf1", [P, SLOTS * H], BF16, "slot_e")
+        for t in range(SLOTS):
+            round_we(1, t)
+        load_gain(1, "slot_d")
+        quantize_we(1, 0, H)
+        wo_raw = sbuf("wo_raw", [P, SLOTS, N], F32, "slot_e")
+        for t in range(SLOTS):
+            nc.sync.dma_start(wo_raw[:, t, :], wo_rows[t])
+        for t in range(SLOTS):
+            excite(t, 0, 1)
+
+        gather_words(2, 0, HALF)
+        we_bf[2] = sbuf("we_bf2", [P, SLOTS * H], BF16)
+        early = [c for c in CHUNKS if c[0] < HALF]
+        late = [c for c in CHUNKS if c[0] >= HALF]
+        h_early = sbuf("h_early", [P, SLOTS, HALF], F32)
+        diff_early = sbuf("diff_early", [P, SLOTS - 1, HALF], F32)
+        diff_last = [sbuf(f"diff_last{k}", [P, c[1]], F32, f"slot_last{k}") for k, c in enumerate(early)]
         for t in range(SLOTS):
             inhibit(t, 0, 2)
             rectify_i(t, 0)
             round_we(2, t)
             quantize_we(2, P * t, P)
             excite(t, 0, 2)
-            subtract(t, 0)
+            if t < SLOTS - 1:
+                subtract(t, 0, HALF, diff_early[:, t, :])
+            else:
+                for k, c in enumerate(early):
+                    subtract(t, c[0], c[1], diff_last[k][:])
             if t == 0:
                 gather_words(2, HALF, HALF)
+                load_gain(2, "slot_a")
             if t < SLOTS - 1:
-                apply_gain(t, 0, HALF)
+                apply_gain(t, 0, HALF, h_early[:, t, :], diff_early[:, t, :])
+        load_gain(3, "slot_b")
 
         for t in range(SLOTS):
             for a in range(PASSES):
@@ -257,17 +273,20 @@ def tile_list_net_drive_trials_kernel(tc, tab_words, tab_scales, offs, we, wi_wo
                 in_=wo_bf[:, 4 * first : 4 * (first + width)],
             )
 
-        chunk_banks = [i_bank[0:2], i_bank[2:4], i_bank[0:2], e_bank[0:1], e_bank[1:2]]
-        for k in range(2):
-            apply_gain(3, CHUNKS[k][0], CHUNKS[k][1])
-        for k in range(2):
-            finish(*CHUNKS[k], chunk_banks[k])
+        chunk_banks = [i_bank[0:2], i_bank[2:4], i_bank[0:2], e_bank[0:1], e_bank[1:3]]
+        for k, c in enumerate(early):
+            apply_gain(3, c[0], c[1], h_early[:, 3, c[0] : c[0] + c[1]], diff_last[k][:])
+        for k, c in enumerate(early):
+            finish(*c, h_early[:, :, c[0] : c[0] + c[1]], chunk_banks[k])
+        n_free = 1
+        diff_free = sbuf("diff_free", [P, n_free, HALF], F32)
+        diff_held = sbuf("diff_held", [P, SLOTS - n_free, HALF], F32, "slot_last0")
+        diff_late = [diff_free[:, t, :] if t < n_free else diff_held[:, t - n_free, :] for t in range(SLOTS)]
         for t in range(SLOTS):
-            subtract(t, 1)
-            if t < 2:
-                apply_gain(t, HALF, HALF)
-        for k in range(2, len(CHUNKS)):
-            for t in range(2, SLOTS):
-                apply_gain(t, CHUNKS[k][0], CHUNKS[k][1])
-        for k in range(2, len(CHUNKS)):
-            finish(*CHUNKS[k], chunk_banks[k])
+            subtract(t, HALF, HALF, diff_late[t])
+        h_late = sbuf("h_late", [P, SLOTS, HALF], F32, "slot_last1")
+        for k, c in enumerate(late):
+            cols = slice(c[0] - HALF, c[0] - HALF + c[1])
+            for t in range(SLOTS):
+                apply_gain(t, c[0], c[1], h_late[:, t, cols], diff_late[t][:, cols])
+            finish(*c, h_late[:, :, cols], chunk_banks[len(early) + k])

@@ -47,9 +47,7 @@ def tile_list_net_drive_trials_kernel(tc, tab_words, tab_scales, offs, we, wi_wo
         wo_bf = sbuf("wo_bf", [P, SLOTS * N], BF16)
         wo_codes = sbuf("wo_codes", [P, N], U32)
         wo_sc = sbuf("wo_sc", [P, N], U8)
-        bias = sbuf("bias", [P, OUT_TILES], F32)
         relu_i = sbuf("relu_i", [P, SLOTS, S], F32)
-        h_bf = sbuf("h_bf", [P, SLOTS * S], BF16)
         h_codes = sbuf("h_codes", [P, S], U32)
         h_sc = sbuf("h_sc", [P, S], U8)
         result = sbuf("result", [P, OUT_TILES, S], F32)
@@ -82,11 +80,12 @@ def tile_list_net_drive_trials_kernel(tc, tab_words, tab_scales, offs, we, wi_wo
             )
 
         def round_we(a, t):
-            nc.scalar.activation(
-                we_bf[a][:, H * t : H * (t + 1)].rearrange("p (w b j) -> p w j b", b=4, j=4),
-                we_raw[a][:].rearrange("p j (w t b) -> p t w j b", t=SLOTS, b=4)[:, t],
-                ACT.Copy,
-            )
+            dst = we_bf[a][:, H * t : H * (t + 1)].rearrange("p (w b j) -> p w j b", b=4, j=4)
+            src = we_raw[a][:].rearrange("p j (w t b) -> p t w j b", t=SLOTS, b=4)[:, t]
+            if (a, t) in ():
+                nc.vector.tensor_copy(dst, src)
+            else:
+                nc.scalar.activation(dst, src, ACT.Copy)
 
         def quantize_we(a, first, width):
             nc.vector.quantize_mx(
@@ -135,9 +134,10 @@ def tile_list_net_drive_trials_kernel(tc, tab_words, tab_scales, offs, we, wi_wo
         def apply_gain(t, first, width, dst, src):
             nc.vector.tensor_tensor(dst, gain[t][:].indirect(picks(first, width)), src, ALU.mult)
 
-        def finish(first, width, round_on, empty_on, h_f32, banks):
+        def finish(first, width, round_on, empty_on, h_f32, banks, slot):
             cols = slice(first, first + width)
-            h_dst = h_bf[:, 4 * first : 4 * (first + width)].rearrange("p (c i t) -> p c t i", i=4, t=SLOTS)
+            h_bf = sbuf(f"h_bf{first}", [P, SLOTS * width], BF16, slot)
+            h_dst = h_bf[:].rearrange("p (c i t) -> p c t i", i=4, t=SLOTS)
             h_src = h_f32.rearrange("p t (c i) -> p c t i", i=4)
             if round_on == "s":
                 nc.scalar.activation(h_dst, h_src, ACT.Copy)
@@ -146,7 +146,7 @@ def tile_list_net_drive_trials_kernel(tc, tab_words, tab_scales, offs, we, wi_wo
             nc.vector.quantize_mx(
                 out=h_codes[:, cols].bitcast(FP8X4),
                 scales=h_sc[:, cols],
-                in_=h_bf[:, 4 * first : 4 * (first + width)],
+                in_=h_bf[:],
             )
             per_bank = -(-OUT_TILES // len(banks))
             sums = [
@@ -187,8 +187,6 @@ def tile_list_net_drive_trials_kernel(tc, tab_words, tab_scales, offs, we, wi_wo
             )
         nc.sync.dma_start(wi_raw[:], wi_words.bitcast(I32).rearrange("a p c -> p a c"))
         load_we(1, "slot_d")
-        with nc.allow_non_contiguous_dma(reason="one bias value for each partition and output tile"):
-            nc.sync.dma_start(bias[:], bo.rearrange("(c p) -> p c", p=P))
 
         gather_words(0, 0, S)
         nc.vector.tensor_copy(v_sc[:], tab_sc[:].bitcast(U8).indirect(picks(0, S)))
@@ -230,7 +228,7 @@ def tile_list_net_drive_trials_kernel(tc, tab_words, tab_scales, offs, we, wi_wo
             excite(t, 0, 1)
 
         gather_words(2, 0, HALF)
-        we_bf[2] = sbuf("we_bf2", [P, SLOTS * H], BF16)
+        we_bf[2] = sbuf("we_bf2", [P, SLOTS * H], BF16, "slot_f")
         early = [c for c in CHUNKS if c[0] < HALF]
         late = [c for c in CHUNKS if c[0] >= HALF]
         h_early = sbuf("h_early", [P, SLOTS, HALF], F32)
@@ -253,6 +251,9 @@ def tile_list_net_drive_trials_kernel(tc, tab_words, tab_scales, offs, we, wi_wo
             if t < SLOTS - 1:
                 apply_gain(t, 0, HALF, h_early[:, t, :], diff_early[:, t, :])
         load_gain(3, "slot_b")
+        bias = sbuf("bias", [P, OUT_TILES], F32, "slot_f")
+        with nc.allow_non_contiguous_dma(reason="one bias value for each partition and output tile"):
+            nc.sync.dma_start(bias[:], bo.rearrange("(c p) -> p c", p=P))
 
         for t in range(SLOTS):
             for a in range(PASSES):
@@ -277,16 +278,18 @@ def tile_list_net_drive_trials_kernel(tc, tab_words, tab_scales, offs, we, wi_wo
         for k, c in enumerate(early):
             apply_gain(3, c[0], c[1], h_early[:, 3, c[0] : c[0] + c[1]], diff_last[k][:])
         for k, c in enumerate(early):
-            finish(*c, h_early[:, :, c[0] : c[0] + c[1]], chunk_banks[k])
+            finish(*c, h_early[:, :, c[0] : c[0] + c[1]], chunk_banks[k], None)
         n_free = 1
         diff_free = sbuf("diff_free", [P, n_free, HALF], F32)
         diff_held = sbuf("diff_held", [P, SLOTS - n_free, HALF], F32, "slot_last0")
         diff_late = [diff_free[:, t, :] if t < n_free else diff_held[:, t - n_free, :] for t in range(SLOTS)]
         for t in range(SLOTS):
             subtract(t, HALF, HALF, diff_late[t])
-        h_late = sbuf("h_late", [P, SLOTS, HALF], F32, "slot_last1")
+        gained_slot = ["slot_last1", None, "slot_g"]
+        rounded_slot = ["slot_g", "slot_h", "slot_h"]
         for k, c in enumerate(late):
             cols = slice(c[0] - HALF, c[0] - HALF + c[1])
+            h_late = sbuf(f"h_late{k}", [P, SLOTS, c[1]], F32, gained_slot[k])
             for t in range(SLOTS):
-                apply_gain(t, c[0], c[1], h_late[:, t, cols], diff_late[t][:, cols])
-            finish(*c, h_late[:, :, cols], chunk_banks[len(early) + k])
+                apply_gain(t, c[0], c[1], h_late[:, t, :], diff_late[t][:, cols])
+            finish(*c, h_late[:], chunk_banks[len(early) + k], rounded_slot[k])

@@ -34,13 +34,13 @@ def tile_list_net_drive_trials_kernel(tc, tab_words, tab_scales, offs, we, wi_wo
             return keep.tile(shape, dtype, name=name, tag=slot or name, align_bytes=64)
 
         offsets = keep.tile([P, S // 16], U16, name="offsets")
-        tab_sc = sbuf("tab_sc", [P, T // 4], I32, "slot_a")
+        tab_sc = sbuf("tab_sc", [P, T // 4], I32, "slot_b")
         v_words = [sbuf(f"v_words{a}", [P, S], U32) for a in range(PASSES)]
         v_sc = sbuf("v_sc", [P, S], U8)
         v_sc_low = sbuf("v_sc_low", [P, PASSES - 1, S], U8)
         we_codes = [sbuf(f"we_codes{a}", [P, H], U32) for a in range(PASSES)]
         we_sc = [sbuf(f"we_sc{a}", [P, H], U8) for a in range(PASSES)]
-        wi_raw = sbuf("wi_raw", [P, PASSES, 2 * H // 4], I32)
+        wi_raw = sbuf("wi_raw", [P, PASSES, 2 * H // 4], I32, "slot_e")
         wi_sc_raw = sbuf("wi_sc_raw", [P, PASSES, H // 4], I32)
         wi_codes = sbuf("wi_codes", [P, SLOTS, PASSES, 2 * P], U8)
         wi_sc = sbuf("wi_sc", [P, SLOTS, PASSES, P], U8)
@@ -187,6 +187,7 @@ def tile_list_net_drive_trials_kernel(tc, tab_words, tab_scales, offs, we, wi_wo
             )
         nc.sync.dma_start(wi_raw[:], wi_words.bitcast(I32).rearrange("a p c -> p a c"))
         load_we(1, "slot_d")
+        load_tab(2, "slot_a")
 
         gather_words(0, 0, S)
         nc.vector.tensor_copy(v_sc[:], tab_sc[:].bitcast(U8).indirect(picks(0, S)))
@@ -194,12 +195,11 @@ def tile_list_net_drive_trials_kernel(tc, tab_words, tab_scales, offs, we, wi_wo
             nc.sync.dma_start(
                 v_sc_low[0:112, a - 1, :].bitcast(I32), v_sc[4 * a : 4 * a + 112, :].bitcast(I32)
             )
-        load_tab(2, "slot_a")
-        we_bf[0] = sbuf("we_bf0", [P, SLOTS * H], BF16, "slot_b")
+        load_we(2, "slot_b")
+        we_bf[0] = sbuf("we_bf0", [P, SLOTS * H], BF16)
         for t in range(SLOTS):
             round_we(0, t)
         quantize_we(0, 0, H)
-        load_we(2, "slot_b")
         for t in range(SLOTS):
             excite(t, 0, 0)
 
@@ -213,17 +213,17 @@ def tile_list_net_drive_trials_kernel(tc, tab_words, tab_scales, offs, we, wi_wo
             wi_sc[:].rearrange("p t a c -> p t (a c)").bitcast(I32),
             wi_sc_raw[:].rearrange("p a (w t) -> p t (a w)", t=SLOTS),
         )
+        wo_raw = sbuf("wo_raw", [P, SLOTS, N], F32, "slot_e")
+        for t in range(SLOTS):
+            nc.sync.dma_start(wo_raw[:, t, :], wo_rows[t])
         for a in range(2):
             for t in range(SLOTS):
                 inhibit(t, 0, a)
-        we_bf[1] = sbuf("we_bf1", [P, SLOTS * H], BF16, "slot_e")
+        we_bf[1] = sbuf("we_bf1", [P, SLOTS * H], BF16)
         for t in range(SLOTS):
             round_we(1, t)
         load_gain(1, "slot_d")
         quantize_we(1, 0, H)
-        wo_raw = sbuf("wo_raw", [P, SLOTS, N], F32, "slot_e")
-        for t in range(SLOTS):
-            nc.sync.dma_start(wo_raw[:, t, :], wo_rows[t])
         for t in range(SLOTS):
             excite(t, 0, 1)
 

@@ -35,7 +35,7 @@ def tile_list_net_drive_trials_kernel(tc, tab_words, tab_scales, offs, we, wi_wo
 
         offsets = keep.tile([P, S // 16], U16, name="offsets")
         tab_sc = sbuf("tab_sc", [P, T // 4], I32, "slot_b")
-        v_words = [sbuf(f"v_words{a}", [P, S], U32) for a in range(PASSES)]
+        v_words = {}
         v_sc = sbuf("v_sc", [P, S], U8)
         v_sc_low = sbuf("v_sc_low", [P, PASSES - 1, S], U8)
         we_codes = [sbuf(f"we_codes{a}", [P, H], U32) for a in range(PASSES)]
@@ -44,16 +44,14 @@ def tile_list_net_drive_trials_kernel(tc, tab_words, tab_scales, offs, we, wi_wo
         wi_sc_raw = sbuf("wi_sc_raw", [P, PASSES, H // 4], I32)
         wi_codes = sbuf("wi_codes", [P, SLOTS, PASSES, 2 * P], U8)
         wi_sc = sbuf("wi_sc", [P, SLOTS, PASSES, P], U8)
-        wo_bf = sbuf("wo_bf", [P, SLOTS * N], BF16)
         wo_codes = sbuf("wo_codes", [P, N], U32)
         wo_sc = sbuf("wo_sc", [P, N], U8)
-        relu_i = sbuf("relu_i", [P, SLOTS, S], F32)
-        h_codes = sbuf("h_codes", [P, S], U32)
-        h_sc = sbuf("h_sc", [P, S], U8)
         result = sbuf("result", [P, OUT_TILES, S], F32)
         i_bank = [psum.tile([P, HALF], F32, name=f"i_bank{t}") for t in range(SLOTS)]
         e_bank = [psum.tile([P, HALF], F32, name=f"e_bank{t}") for t in range(SLOTS)]
-        tab, we_raw, we_bf, gain = {}, {}, {}, {}
+        bank_sets = [e_bank, i_bank]
+        pass_order = [(0, 1, 2), (2, 0, 1)]
+        tab, we_raw, we_bf, gain, relu_i = {}, {}, {}, {}, {}
 
         gain_rows = gT.rearrange("(w t b) c -> t w b c", t=SLOTS, b=4)
         wo_rows = wo.rearrange("(w t b) n -> t w b n", t=SLOTS, b=4)
@@ -74,59 +72,62 @@ def tile_list_net_drive_trials_kernel(tc, tab_words, tab_scales, offs, we, wi_wo
             gain[t] = sbuf(f"gain{t}", [P, T], F32, slot)
             nc.sync.dma_start(gain[t][:], gain_rows[t])
 
-        def gather_words(a, first, width):
-            nc.vector.tensor_copy(
-                v_words[a][:, first : first + width], tab[a][:].bitcast(U32).indirect(picks(first, width))
-            )
+        def gather_words(a, first, width, slot=None):
+            picked = sbuf(f"v_words{a}_{first}", [P, width], U32, slot)
+            nc.vector.tensor_copy(picked[:], tab[a][:].bitcast(U32).indirect(picks(first, width)))
+            for half in range(first // HALF, (first + width) // HALF):
+                v_words[a, half] = picked[:, HALF * half - first : HALF * (half + 1) - first]
 
-        def round_we(a, t):
-            dst = we_bf[a][:, H * t : H * (t + 1)].rearrange("p (w b j) -> p w j b", b=4, j=4)
+        def round_we(a, t, rounded, on_vector):
+            dst = rounded.rearrange("p (w b j) -> p w j b", b=4, j=4)
             src = we_raw[a][:].rearrange("p j (w t b) -> p t w j b", t=SLOTS, b=4)[:, t]
-            if (a, t) in ():
+            if on_vector:
                 nc.vector.tensor_copy(dst, src)
             else:
                 nc.scalar.activation(dst, src, ACT.Copy)
 
-        def quantize_we(a, first, width):
+        def quantize_we(a, first, width, rounded):
             nc.vector.quantize_mx(
                 out=we_codes[a][:, first : first + width].bitcast(FP8X4),
                 scales=we_sc[a][:, first : first + width],
-                in_=we_bf[a][:, 4 * first : 4 * (first + width)],
+                in_=rounded,
             )
 
         def excite(t, half, a):
             cols = slice(HALF * half, HALF * (half + 1))
+            order = pass_order[half]
             nc.tensor.matmul_mx(
-                out=e_bank[t][:],
+                out=bank_sets[half][t][:],
                 lhsT=we_codes[a][:, P * t : P * (t + 1)].bitcast(FP8X4),
                 lhsT_scale=we_sc[a][:, P * t : P * (t + 1)],
-                rhs=v_words[a][:, cols].bitcast(FP8X4),
+                rhs=v_words[a, half].bitcast(FP8X4),
                 rhs_scale=v_sc[4 * a :, cols],
-                start=(a == 0),
-                stop=(a == PASSES - 1),
+                start=(a == order[0]),
+                stop=(a == order[-1]),
             )
 
         def inhibit(t, half, a):
             cols = slice(HALF * half, HALF * (half + 1))
             nc.tensor.matmul_mx(
-                out=i_bank[t][:],
+                out=bank_sets[1 - half][t][:],
                 lhsT=wi_codes[:, t, a, :].bitcast(FP4X4),
                 lhsT_scale=wi_sc[:, t, a, :],
-                rhs=v_words[a][:, cols].bitcast(FP8X4),
+                rhs=v_words[a, half].bitcast(FP8X4),
                 rhs_scale=v_sc[:, cols] if a == 0 else v_sc_low[:, a - 1, cols],
                 start=(a == 0),
                 stop=(a == PASSES - 1),
             )
 
-        def rectify_i(t, half):
-            nc.scalar.activation(relu_i[:, t, HALF * half : HALF * (half + 1)], i_bank[t][:], ACT.Relu)
+        def rectify_i(t, half, slot):
+            relu_i[t, half] = sbuf(f"relu_i{t}_{half}", [P, HALF], F32, slot)
+            nc.scalar.activation(relu_i[t, half][:], bank_sets[1 - half][t][:], ACT.Relu)
 
         def subtract(t, first, width, dst):
             nc.vector.scalar_tensor_tensor(
                 dst,
-                e_bank[t][:, first % HALF : first % HALF + width],
+                bank_sets[first // HALF][t][:, first % HALF : first % HALF + width],
                 0.0,
-                relu_i[:, t, first : first + width],
+                relu_i[t, first // HALF][:, first % HALF : first % HALF + width],
                 ALU.max,
                 ALU.subtract,
             )
@@ -134,9 +135,10 @@ def tile_list_net_drive_trials_kernel(tc, tab_words, tab_scales, offs, we, wi_wo
         def apply_gain(t, first, width, dst, src):
             nc.vector.tensor_tensor(dst, gain[t][:].indirect(picks(first, width)), src, ALU.mult)
 
-        def finish(first, width, round_on, empty_on, h_f32, banks, slot):
-            cols = slice(first, first + width)
-            h_bf = sbuf(f"h_bf{first}", [P, SLOTS * width], BF16, slot)
+        def quantize_h(first, width, round_on, h_f32):
+            h_bf = sbuf(f"h_bf{first}", [P, SLOTS * width], BF16)
+            h_codes = sbuf(f"h_codes{first}", [P, width], U32)
+            h_sc = sbuf(f"h_sc{first}", [P, width], U8)
             h_dst = h_bf[:].rearrange("p (c i t) -> p c t i", i=4, t=SLOTS)
             h_src = h_f32.rearrange("p t (c i) -> p c t i", i=4)
             if round_on == "s":
@@ -144,10 +146,14 @@ def tile_list_net_drive_trials_kernel(tc, tab_words, tab_scales, offs, we, wi_wo
             else:
                 nc.vector.tensor_copy(h_dst, h_src)
             nc.vector.quantize_mx(
-                out=h_codes[:, cols].bitcast(FP8X4),
-                scales=h_sc[:, cols],
+                out=h_codes[:].bitcast(FP8X4),
+                scales=h_sc[:],
                 in_=h_bf[:],
             )
+            return h_codes, h_sc
+
+        def emit(first, width, empty_on, h_codes, h_sc, banks):
+            cols = slice(first, first + width)
             per_bank = -(-OUT_TILES // len(banks))
             sums = [
                 banks[c // per_bank][:, width * (c % per_bank) : width * (c % per_bank + 1)] for c in range(OUT_TILES)
@@ -157,8 +163,8 @@ def tile_list_net_drive_trials_kernel(tc, tab_words, tab_scales, offs, we, wi_wo
                     out=sums[c],
                     lhsT=wo_codes[:, P * c : P * (c + 1)].bitcast(FP8X4),
                     lhsT_scale=wo_sc[:, P * c : P * (c + 1)],
-                    rhs=h_codes[:, cols].bitcast(FP8X4),
-                    rhs_scale=h_sc[:, cols],
+                    rhs=h_codes[:].bitcast(FP8X4),
+                    rhs_scale=h_sc[:],
                     start=True,
                     stop=True,
                 )
@@ -198,13 +204,11 @@ def tile_list_net_drive_trials_kernel(tc, tab_words, tab_scales, offs, we, wi_wo
         load_we(2, "slot_b")
         we_bf[0] = sbuf("we_bf0", [P, SLOTS * H], BF16)
         for t in range(SLOTS):
-            round_we(0, t)
-        quantize_we(0, 0, H)
+            round_we(0, t, we_bf[0][:, H * t : H * (t + 1)], False)
+        quantize_we(0, 0, H, we_bf[0][:])
         for t in range(SLOTS):
             excite(t, 0, 0)
 
-        gather_words(1, 0, S)
-        load_gain(0, "slot_c")
         nc.vector.tensor_copy(
             wi_codes[:].rearrange("p t a c -> p t (a c)").bitcast(I32).rearrange("p t (u e) -> p t u e", e=2),
             wi_raw[:].rearrange("p a (w t e) -> p t (a w) e", t=SLOTS, e=2),
@@ -213,55 +217,62 @@ def tile_list_net_drive_trials_kernel(tc, tab_words, tab_scales, offs, we, wi_wo
             wi_sc[:].rearrange("p t a c -> p t (a c)").bitcast(I32),
             wi_sc_raw[:].rearrange("p a (w t) -> p t (a w)", t=SLOTS),
         )
-        wo_raw = sbuf("wo_raw", [P, SLOTS, N], F32, "slot_e")
-        for t in range(SLOTS):
-            nc.sync.dma_start(wo_raw[:, t, :], wo_rows[t])
+
+        gather_words(1, 0, S)
+        load_gain(0, "slot_c")
         for a in range(2):
             for t in range(SLOTS):
                 inhibit(t, 0, a)
-        we_bf[1] = sbuf("we_bf1", [P, SLOTS * H], BF16)
+        we_bf[1] = sbuf("we_bf1", [P, SLOTS * H], BF16, "slot_g")
         for t in range(SLOTS):
-            round_we(1, t)
-        load_gain(1, "slot_d")
-        quantize_we(1, 0, H)
+            round_we(1, t, we_bf[1][:, H * t : H * (t + 1)], False)
+        wo_raw = sbuf("wo_raw", [P, SLOTS, N], F32, "slot_d")
         for t in range(SLOTS):
-            excite(t, 0, 1)
+            nc.sync.dma_start(wo_raw[:, t, :], wo_rows[t])
+        quantize_we(1, 0, H, we_bf[1][:])
 
         gather_words(2, 0, HALF)
-        we_bf[2] = sbuf("we_bf2", [P, SLOTS * H], BF16, "slot_f")
+        gather_words(2, HALF, HALF)
+        load_gain(1, "slot_a")
         early = [c for c in CHUNKS if c[0] < HALF]
         late = [c for c in CHUNKS if c[0] >= HALF]
         h_early = sbuf("h_early", [P, SLOTS, HALF], F32)
-        diff_early = sbuf("diff_early", [P, SLOTS - 1, HALF], F32)
+        diff_early = [sbuf(f"diff_early{t}", [P, HALF], F32) for t in range(SLOTS - 1)]
         diff_last = [sbuf(f"diff_last{k}", [P, c[1]], F32, f"slot_last{k}") for k, c in enumerate(early)]
         for t in range(SLOTS):
             inhibit(t, 0, 2)
-            rectify_i(t, 0)
-            round_we(2, t)
-            quantize_we(2, P * t, P)
+        for t in range(SLOTS):
+            excite(t, 0, 1)
+        for t in range(SLOTS):
+            rounded = sbuf(f"we_bf2_{t}", [P, H], BF16, f"slot_r{t}")
+            round_we(2, t, rounded[:], False)
+            quantize_we(2, P * t, P, rounded[:])
+            if t == 0:
+                load_gain(2, "slot_r0")
             excite(t, 0, 2)
+            rectify_i(t, 0, f"slot_r{t}" if t > 0 else None)
             if t < SLOTS - 1:
-                subtract(t, 0, HALF, diff_early[:, t, :])
+                subtract(t, 0, HALF, diff_early[t][:])
+                apply_gain(t, 0, HALF, h_early[:, t, :], diff_early[t][:])
             else:
                 for k, c in enumerate(early):
                     subtract(t, c[0], c[1], diff_last[k][:])
-            if t == 0:
-                gather_words(2, HALF, HALF)
-                load_gain(2, "slot_a")
-            if t < SLOTS - 1:
-                apply_gain(t, 0, HALF, h_early[:, t, :], diff_early[:, t, :])
-        load_gain(3, "slot_b")
-        bias = sbuf("bias", [P, OUT_TILES], F32, "slot_f")
+        bias = sbuf("bias", [P, OUT_TILES], F32, "diff_early0")
         with nc.allow_non_contiguous_dma(reason="one bias value for each partition and output tile"):
             nc.sync.dma_start(bias[:], bo.rearrange("(c p) -> p c", p=P))
+        load_gain(3, "slot_b")
 
-        for t in range(SLOTS):
+        def second_half_sums(t):
+            for a in pass_order[1]:
+                excite(t, 1, a)
             for a in range(PASSES):
                 inhibit(t, 1, a)
-            rectify_i(t, 1)
-            for a in range(PASSES):
-                excite(t, 1, a)
+            rectify_i(t, 1, None)
 
+        for t in range(SLOTS):
+            second_half_sums(t)
+
+        wo_bf = sbuf("wo_bf", [P, SLOTS * N], BF16)
         nc.scalar.activation(
             wo_bf[:].rearrange("p (c i t) -> p c t i", i=4, t=SLOTS),
             wo_raw[:].rearrange("p t (c i) -> p c t i", i=4),
@@ -274,22 +285,28 @@ def tile_list_net_drive_trials_kernel(tc, tab_words, tab_scales, offs, we, wi_wo
                 in_=wo_bf[:, 4 * first : 4 * (first + width)],
             )
 
-        chunk_banks = [i_bank[0:2], i_bank[2:4], i_bank[0:2], e_bank[0:1], e_bank[1:3]]
+        n_free = 1
+        mid, tail = late[0], late[1:]
+        diff_free = sbuf("diff_free", [P, n_free, HALF], F32)
+        h_mid = sbuf("h_mid", [P, SLOTS, mid[1]], F32)
+        for t in range(n_free):
+            subtract(t, HALF, HALF, diff_free[:, t, :])
+            apply_gain(t, HALF, mid[1], h_mid[:, t, :], diff_free[:, t, : mid[1]])
         for k, c in enumerate(early):
             apply_gain(3, c[0], c[1], h_early[:, 3, c[0] : c[0] + c[1]], diff_last[k][:])
-        for k, c in enumerate(early):
-            finish(*c, h_early[:, :, c[0] : c[0] + c[1]], chunk_banks[k], None)
-        n_free = 1
-        diff_free = sbuf("diff_free", [P, n_free, HALF], F32)
+        made = [quantize_h(c[0], c[1], c[2], h_early[:, :, c[0] : c[0] + c[1]]) for c in early]
         diff_held = sbuf("diff_held", [P, SLOTS - n_free, HALF], F32, "slot_last0")
         diff_late = [diff_free[:, t, :] if t < n_free else diff_held[:, t - n_free, :] for t in range(SLOTS)]
-        for t in range(SLOTS):
+        for t in range(n_free, SLOTS):
             subtract(t, HALF, HALF, diff_late[t])
-        gained_slot = ["slot_last1", None, "slot_g"]
-        rounded_slot = ["slot_g", "slot_h", "slot_h"]
-        for k, c in enumerate(late):
-            cols = slice(c[0] - HALF, c[0] - HALF + c[1])
-            h_late = sbuf(f"h_late{k}", [P, SLOTS, c[1]], F32, gained_slot[k])
+        for t in range(n_free, SLOTS):
+            apply_gain(t, HALF, mid[1], h_mid[:, t, :], diff_late[t][:, : mid[1]])
+        emit(early[0][0], early[0][1], early[0][3], *made[0], e_bank[0:2])
+        made.append(quantize_h(mid[0], mid[1], mid[2], h_mid[:]))
+        emit(early[1][0], early[1][1], early[1][3], *made[1], e_bank[2:4])
+        emit(mid[0], mid[1], mid[3], *made[2], e_bank[0:2])
+        for k, c in enumerate(tail):
+            h_tail = sbuf(f"h_tail{k}", [P, SLOTS, c[1]], F32, ("h_bf0", "h_bf512")[k])
             for t in range(SLOTS):
-                apply_gain(t, c[0], c[1], h_late[:, t, :], diff_late[t][:, cols])
-            finish(*c, h_late[:], chunk_banks[len(early) + k], rounded_slot[k])
+                apply_gain(t, c[0], c[1], h_tail[:, t, :], diff_late[t][:, c[0] - HALF : c[0] - HALF + c[1]])
+            emit(c[0], c[1], c[3], *quantize_h(c[0], c[1], c[2], h_tail[:]), (i_bank[0:1], i_bank[1:3])[k])

@@ -21,7 +21,7 @@ PASSES = K // 512
 SLOTS = 4
 HALF = 512
 OUT_TILES = N // P
-CHUNKS = [(0, 256, "s", "sss"), (256, 256, "s", "sss"), (512, 256, "s", "sss"), (768, 128, "s", "sss"), (896, 128, "v", "vvs")]
+CHUNKS = [(0, 256, "s", "sss"), (256, 256, "s", "sss"), (512, 256, "s", "sss"), (768, 128, "s", "sss"), (896, 128, "v", "svs")]
 
 
 def tile_list_net_drive_trials_kernel(tc, tab_words, tab_scales, offs, we, wi_words, wi_scales, gT, wo, bo, out):
@@ -186,10 +186,10 @@ def tile_list_net_drive_trials_kernel(tc, tab_words, tab_scales, offs, we, wi_wo
                 tab_sc[32 * q : 32 * q + 4 * PASSES, :], tab_scales[:, 4 * q : 4 * q + 4, :].bitcast(I32)
             )
         load_tab(1, "slot_c")
-        for q in range(4):
+        for r in range(4):
             nc.sync.dma_start(
-                wi_sc_raw[32 * q : 32 * q + 4, :, :],
-                wi_scales[:, 4 * q : 4 * q + 4, :].bitcast(I32).rearrange("a r c -> r a c"),
+                wi_sc_raw[r:P:32, :, :],
+                wi_scales.bitcast(I32).rearrange("a (q r) c -> r q a c", r=4)[r],
             )
         nc.sync.dma_start(wi_raw[:], wi_words.bitcast(I32).rearrange("a p c -> p a c"))
         load_we(1, "slot_d")
@@ -257,10 +257,10 @@ def tile_list_net_drive_trials_kernel(tc, tab_words, tab_scales, offs, we, wi_wo
             else:
                 for k, c in enumerate(early):
                     subtract(t, c[0], c[1], diff_last[k][:])
+        load_gain(3, "slot_b")
         bias = sbuf("bias", [P, OUT_TILES], F32, "diff_early0")
         with nc.allow_non_contiguous_dma(reason="one bias value for each partition and output tile"):
             nc.sync.dma_start(bias[:], bo.rearrange("(c p) -> p c", p=P))
-        load_gain(3, "slot_b")
 
         def second_half_sums(t):
             for a in pass_order[1]:
@@ -297,16 +297,24 @@ def tile_list_net_drive_trials_kernel(tc, tab_words, tab_scales, offs, we, wi_wo
         made = [quantize_h(c[0], c[1], c[2], h_early[:, :, c[0] : c[0] + c[1]]) for c in early]
         diff_held = sbuf("diff_held", [P, SLOTS - n_free, HALF], F32, "slot_last0")
         diff_late = [diff_free[:, t, :] if t < n_free else diff_held[:, t - n_free, :] for t in range(SLOTS)]
+        last = HALF - tail[-1][1]
         for t in range(n_free, SLOTS):
-            subtract(t, HALF, HALF, diff_late[t])
+            subtract(t, HALF, last, diff_late[t][:, :last])
         for t in range(n_free, SLOTS):
             apply_gain(t, HALF, mid[1], h_mid[:, t, :], diff_late[t][:, : mid[1]])
         emit(early[0][0], early[0][1], early[0][3], *made[0], e_bank[0:2])
         made.append(quantize_h(mid[0], mid[1], mid[2], h_mid[:]))
-        emit(early[1][0], early[1][1], early[1][3], *made[1], e_bank[2:4])
-        emit(mid[0], mid[1], mid[3], *made[2], e_bank[0:2])
-        for k, c in enumerate(tail):
-            h_tail = sbuf(f"h_tail{k}", [P, SLOTS, c[1]], F32, ("h_bf0", "h_bf512")[k])
+
+        def gains_and_codes(c, slot):
+            h_tail = sbuf(f"h_tail{c[0]}", [P, SLOTS, c[1]], F32, slot)
             for t in range(SLOTS):
                 apply_gain(t, c[0], c[1], h_tail[:, t, :], diff_late[t][:, c[0] - HALF : c[0] - HALF + c[1]])
-            emit(c[0], c[1], c[3], *quantize_h(c[0], c[1], c[2], h_tail[:]), (i_bank[0:1], i_bank[1:3])[k])
+            return quantize_h(c[0], c[1], c[2], h_tail[:])
+
+        made.append(gains_and_codes(tail[0], "h_bf0"))
+        emit(early[1][0], early[1][1], early[1][3], *made[1], e_bank[2:4])
+        emit(mid[0], mid[1], mid[3], *made[2], e_bank[0:2])
+        emit(tail[0][0], tail[0][1], tail[0][3], *made[3], i_bank[0:1])
+        for t in range(n_free, SLOTS):
+            subtract(t, tail[1][0], tail[1][1], diff_late[t][:, last:])
+        emit(tail[1][0], tail[1][1], tail[1][3], *gains_and_codes(tail[1], "h_mid"), i_bank[1:4])

@@ -220,12 +220,11 @@ def tile_list_net_drive_trials_kernel(tc, tab_words, tab_scales, offs, we, wi_wo
 
         gather_words(1, 0, S)
         load_gain(0, "slot_c")
-        for a in range(2):
-            for t in range(SLOTS):
-                inhibit(t, 0, a)
+        for t in range(SLOTS):
+            inhibit(t, 0, 0)
         we_bf[1] = sbuf("we_bf1", [P, SLOTS * H], BF16, "slot_g")
         for t in range(SLOTS):
-            round_we(1, t, we_bf[1][:, H * t : H * (t + 1)], False)
+            round_we(1, t, we_bf[1][:, H * t : H * (t + 1)], t >= 2)
         wo_raw = sbuf("wo_raw", [P, SLOTS, N], F32, "slot_d")
         for t in range(SLOTS):
             nc.sync.dma_start(wo_raw[:, t, :], wo_rows[t])
@@ -240,12 +239,13 @@ def tile_list_net_drive_trials_kernel(tc, tab_words, tab_scales, offs, we, wi_wo
         diff_early = [sbuf(f"diff_early{t}", [P, HALF], F32) for t in range(SLOTS - 1)]
         diff_last = [sbuf(f"diff_last{k}", [P, c[1]], F32, f"slot_last{k}") for k, c in enumerate(early)]
         for t in range(SLOTS):
-            inhibit(t, 0, 2)
+            for a in range(1, PASSES):
+                inhibit(t, 0, a)
         for t in range(SLOTS):
             excite(t, 0, 1)
         for t in range(SLOTS):
             rounded = sbuf(f"we_bf2_{t}", [P, H], BF16, f"slot_r{t}")
-            round_we(2, t, rounded[:], False)
+            round_we(2, t, rounded[:], t < SLOTS - 1)
             quantize_we(2, P * t, P, rounded[:])
             if t == 0:
                 load_gain(2, "slot_r0")

@@ -34,7 +34,7 @@ def tile_list_net_drive_trials_kernel(tc, tab_words, tab_scales, offs, we, wi_wo
             return keep.tile(shape, dtype, name=name, tag=slot or name, align_bytes=64)
 
         offsets = keep.tile([P, S // 16], U16, name="offsets")
-        tab_sc = sbuf("tab_sc", [P, T // 4], I32, "slot_b")
+        tab_sc = sbuf("tab_sc", [P, T // 4], I32)
         v_words = {}
         v_sc = sbuf("v_sc", [P, S], U8)
         v_sc_low = sbuf("v_sc_low", [P, PASSES - 1, S], U8)
@@ -185,8 +185,13 @@ def tile_list_net_drive_trials_kernel(tc, tab_words, tab_scales, offs, we, wi_wo
             nc.sync.dma_start(
                 tab_sc[32 * q : 32 * q + 4 * PASSES, :], tab_scales[:, 4 * q : 4 * q + 4, :].bitcast(I32)
             )
+        for r in range(2):
+            nc.sync.dma_start(
+                wi_sc_raw[r:P:32, :, :],
+                wi_scales.bitcast(I32).rearrange("a (q r) c -> r q a c", r=4)[r],
+            )
         load_tab(1, "slot_c")
-        for r in range(4):
+        for r in range(2, 4):
             nc.sync.dma_start(
                 wi_sc_raw[r:P:32, :, :],
                 wi_scales.bitcast(I32).rearrange("a (q r) c -> r q a c", r=4)[r],
@@ -194,14 +199,14 @@ def tile_list_net_drive_trials_kernel(tc, tab_words, tab_scales, offs, we, wi_wo
         nc.sync.dma_start(wi_raw[:], wi_words.bitcast(I32).rearrange("a p c -> p a c"))
         load_we(1, "slot_d")
         load_tab(2, "slot_a")
+        load_we(2, "slot_b")
 
         gather_words(0, 0, S)
         nc.vector.tensor_copy(v_sc[:], tab_sc[:].bitcast(U8).indirect(picks(0, S)))
         for a in range(1, PASSES):
-            nc.sync.dma_start(
+            nc.scalar.dma_start(
                 v_sc_low[0:112, a - 1, :].bitcast(I32), v_sc[4 * a : 4 * a + 112, :].bitcast(I32)
             )
-        load_we(2, "slot_b")
         we_bf[0] = sbuf("we_bf0", [P, SLOTS * H], BF16)
         for t in range(SLOTS):
             round_we(0, t, we_bf[0][:, H * t : H * (t + 1)], False)

@@ -21,7 +21,7 @@ PASSES = K // 512
 SLOTS = 4
 HALF = 512
 OUT_TILES = N // P
-CHUNKS = [(0, 256, "s", "sss"), (256, 256, "s", "sss"), (512, 256, "s", "sss"), (768, 128, "s", "sss"), (896, 128, "v", "svs")]
+BANKS = 8
 
 
 def tile_list_net_drive_trials_kernel(tc, tab_words, tab_scales, offs, we, wi_words, wi_scales, gT, wo, bo, out):
@@ -34,24 +34,28 @@ def tile_list_net_drive_trials_kernel(tc, tab_words, tab_scales, offs, we, wi_wo
             return keep.tile(shape, dtype, name=name, tag=slot or name, align_bytes=64)
 
         offsets = keep.tile([P, S // 16], U16, name="offsets")
-        tab_sc = sbuf("tab_sc", [P, T // 4], I32)
-        v_words = {}
-        v_sc = sbuf("v_sc", [P, S], U8)
-        v_sc_low = sbuf("v_sc_low", [P, PASSES - 1, S], U8)
+        tab_sc = sbuf("tab_sc", [P, T // 4], I32, "slot_sc")
+        picked_sc = sbuf("picked_sc", [P, S], U8)
+        v_sc_early = sbuf("v_sc_early", [P, 2, S], U8)
+        v_sc_last = sbuf("v_sc_last", [P, S], U8)
+        v_sc = [v_sc_early[:, 0, :], v_sc_early[:, 1, :], v_sc_last[:]]
         we_codes = [sbuf(f"we_codes{a}", [P, H], U32) for a in range(PASSES)]
         we_sc = [sbuf(f"we_sc{a}", [P, H], U8) for a in range(PASSES)]
-        wi_raw = sbuf("wi_raw", [P, PASSES, 2 * H // 4], I32, "slot_e")
+        wi_raw = sbuf("wi_raw", [P, PASSES, 2 * H // 4], I32)
         wi_sc_raw = sbuf("wi_sc_raw", [P, PASSES, H // 4], I32)
-        wi_codes = sbuf("wi_codes", [P, SLOTS, PASSES, 2 * P], U8)
         wi_sc = sbuf("wi_sc", [P, SLOTS, PASSES, P], U8)
+        wo_raw = sbuf("wo_raw", [P, SLOTS, N], F32)
+        wo_bf = sbuf("wo_bf", [P, SLOTS * N], BF16)
         wo_codes = sbuf("wo_codes", [P, N], U32)
         wo_sc = sbuf("wo_sc", [P, N], U8)
+        bias = sbuf("bias", [P, OUT_TILES], F32)
         result = sbuf("result", [P, OUT_TILES, S], F32)
-        i_bank = [psum.tile([P, HALF], F32, name=f"i_bank{t}") for t in range(SLOTS)]
-        e_bank = [psum.tile([P, HALF], F32, name=f"e_bank{t}") for t in range(SLOTS)]
-        bank_sets = [e_bank, i_bank]
-        pass_order = [(0, 1, 2), (2, 0, 1)]
-        tab, we_raw, we_bf, gain, relu_i = {}, {}, {}, {}, {}
+        tab = [sbuf(f"tab{a}", [P, T], I32) for a in range(PASSES)]
+        we_raw = [sbuf(f"we_raw{a}", [P, SLOTS, H], F32) for a in range(PASSES)]
+        gain = [sbuf(f"gain{t}", [P, T], F32) for t in range(SLOTS)]
+        banks = [psum.tile([P, HALF], F32, name=f"bank{b}") for b in range(BANKS)]
+        i_bank, e_bank = banks[:SLOTS], banks[SLOTS:]
+        v_words, relu_i, diff = {}, {}, {}
 
         gain_rows = gT.rearrange("(w t b) c -> t w b c", t=SLOTS, b=4)
         wo_rows = wo.rearrange("(w t b) n -> t w b n", t=SLOTS, b=4)
@@ -60,104 +64,84 @@ def tile_list_net_drive_trials_kernel(tc, tab_words, tab_scales, offs, we, wi_wo
         def picks(first, width):
             return offsets[:, first // 16 : (first + width) // 16]
 
-        def load_tab(a, slot):
-            tab[a] = sbuf(f"tab{a}", [P, T], I32, slot)
+        def load_tab(a):
             nc.sync.dma_start(tab[a][:], tab_words[a].rearrange("p t i -> p (t i)").bitcast(I32))
 
-        def load_we(a, slot):
-            we_raw[a] = sbuf(f"we_raw{a}", [P, SLOTS, H], F32, slot)
+        def load_we(a):
             nc.sync.dma_start(we_raw[a][:], we[512 * a : 512 * (a + 1), :].rearrange("(p j) r -> p j r", j=4))
 
-        def load_gain(t, slot):
-            gain[t] = sbuf(f"gain{t}", [P, T], F32, slot)
+        def load_gain(t):
             nc.sync.dma_start(gain[t][:], gain_rows[t])
 
-        def gather_words(a, first, width, slot=None):
-            picked = sbuf(f"v_words{a}_{first}", [P, width], U32, slot)
+        def gather_words(a, first, width):
+            picked = sbuf(f"v_words{a}_{first}", [P, width], U32)
             nc.vector.tensor_copy(picked[:], tab[a][:].bitcast(U32).indirect(picks(first, width)))
             for half in range(first // HALF, (first + width) // HALF):
                 v_words[a, half] = picked[:, HALF * half - first : HALF * (half + 1) - first]
 
-        def round_we(a, t, rounded, on_vector):
-            dst = rounded.rearrange("p (w b j) -> p w j b", b=4, j=4)
-            src = we_raw[a][:].rearrange("p j (w t b) -> p t w j b", t=SLOTS, b=4)[:, t]
+        def round_we(a, t, count, rounded, on_vector):
+            dst = rounded.rearrange("p (t w b j) -> p t w j b", t=count, b=4, j=4)
+            src = we_raw[a][:].rearrange("p j (w t b) -> p t w j b", t=SLOTS, b=4)[:, t : t + count]
             if on_vector:
                 nc.vector.tensor_copy(dst, src)
             else:
-                nc.scalar.activation(dst, src, ACT.Copy)
+                for u in range(count):
+                    nc.scalar.activation(dst[:, u], src[:, u], ACT.Copy)
 
-        def quantize_we(a, first, width, rounded):
-            nc.vector.quantize_mx(
-                out=we_codes[a][:, first : first + width].bitcast(FP8X4),
-                scales=we_sc[a][:, first : first + width],
-                in_=rounded,
-            )
+        def quantize_we(a, t, count, rounded):
+            cols = slice(P * t, P * (t + count))
+            nc.vector.quantize_mx(out=we_codes[a][:, cols].bitcast(FP8X4), scales=we_sc[a][:, cols], in_=rounded)
 
         def excite(t, half, a):
-            cols = slice(HALF * half, HALF * (half + 1))
-            order = pass_order[half]
             nc.tensor.matmul_mx(
-                out=bank_sets[half][t][:],
+                out=e_bank[t][:],
                 lhsT=we_codes[a][:, P * t : P * (t + 1)].bitcast(FP8X4),
                 lhsT_scale=we_sc[a][:, P * t : P * (t + 1)],
                 rhs=v_words[a, half].bitcast(FP8X4),
-                rhs_scale=v_sc[4 * a :, cols],
-                start=(a == order[0]),
-                stop=(a == order[-1]),
-            )
-
-        def inhibit(t, half, a):
-            cols = slice(HALF * half, HALF * (half + 1))
-            nc.tensor.matmul_mx(
-                out=bank_sets[1 - half][t][:],
-                lhsT=wi_codes[:, t, a, :].bitcast(FP4X4),
-                lhsT_scale=wi_sc[:, t, a, :],
-                rhs=v_words[a, half].bitcast(FP8X4),
-                rhs_scale=v_sc[:, cols] if a == 0 else v_sc_low[:, a - 1, cols],
+                rhs_scale=v_sc[a][:, HALF * half : HALF * (half + 1)],
                 start=(a == 0),
                 stop=(a == PASSES - 1),
             )
 
-        def rectify_i(t, half, slot):
-            relu_i[t, half] = sbuf(f"relu_i{t}_{half}", [P, HALF], F32, slot)
-            nc.scalar.activation(relu_i[t, half][:], bank_sets[1 - half][t][:], ACT.Relu)
+        def inhibit(t, half, a):
+            nc.tensor.matmul_mx(
+                out=i_bank[t][:],
+                lhsT=wi_codes[:, t, a, :].bitcast(FP4X4),
+                lhsT_scale=wi_sc[:, t, a, :],
+                rhs=v_words[a, half].bitcast(FP8X4),
+                rhs_scale=v_sc[a][:, HALF * half : HALF * (half + 1)],
+                start=(a == 0),
+                stop=(a == PASSES - 1),
+            )
 
-        def subtract(t, first, width, dst):
+        def rectify_i(t, half, slot=None):
+            relu_i[t, half] = sbuf(f"relu_i{t}_{half}", [P, HALF], F32, slot)
+            nc.scalar.activation(relu_i[t, half][:], i_bank[t][:], ACT.Relu)
+
+        def subtract(t, half):
+            diff[t, half] = sbuf(f"diff{t}_{half}", [P, HALF], F32)
             nc.vector.scalar_tensor_tensor(
-                dst,
-                bank_sets[first // HALF][t][:, first % HALF : first % HALF + width],
-                0.0,
-                relu_i[t, first // HALF][:, first % HALF : first % HALF + width],
-                ALU.max,
-                ALU.subtract,
+                diff[t, half][:], e_bank[t][:], 0.0, relu_i[t, half][:], ALU.max, ALU.subtract
             )
 
         def apply_gain(t, first, width, dst, src):
             nc.vector.tensor_tensor(dst, gain[t][:].indirect(picks(first, width)), src, ALU.mult)
 
-        def quantize_h(first, width, round_on, h_f32):
+        def round_h(first, width, on_vector, h_f32):
             h_bf = sbuf(f"h_bf{first}", [P, SLOTS * width], BF16)
-            h_codes = sbuf(f"h_codes{first}", [P, width], U32)
-            h_sc = sbuf(f"h_sc{first}", [P, width], U8)
             h_dst = h_bf[:].rearrange("p (c i t) -> p c t i", i=4, t=SLOTS)
             h_src = h_f32.rearrange("p t (c i) -> p c t i", i=4)
-            if round_on == "s":
-                nc.scalar.activation(h_dst, h_src, ACT.Copy)
-            else:
+            if on_vector:
                 nc.vector.tensor_copy(h_dst, h_src)
-            nc.vector.quantize_mx(
-                out=h_codes[:].bitcast(FP8X4),
-                scales=h_sc[:],
-                in_=h_bf[:],
-            )
-            return h_codes, h_sc
+            else:
+                nc.scalar.activation(h_dst, h_src, ACT.Copy)
+            return h_bf
 
-        def emit(first, width, empty_on, h_codes, h_sc, banks):
-            cols = slice(first, first + width)
-            per_bank = -(-OUT_TILES // len(banks))
-            sums = [
-                banks[c // per_bank][:, width * (c % per_bank) : width * (c % per_bank + 1)] for c in range(OUT_TILES)
-            ]
+        def product(chunk, first, width, h_bf):
+            h_codes = sbuf(f"h_codes{first}", [P, width], U32)
+            h_sc = sbuf(f"h_sc{first}", [P, width], U8)
+            nc.vector.quantize_mx(out=h_codes[:].bitcast(FP8X4), scales=h_sc[:], in_=h_bf[:])
+            sums = [banks[(OUT_TILES * chunk + c) % BANKS][:, :width] for c in range(OUT_TILES)]
             for c in range(OUT_TILES):
                 nc.tensor.matmul_mx(
                     out=sums[c],
@@ -168,6 +152,10 @@ def tile_list_net_drive_trials_kernel(tc, tab_words, tab_scales, offs, we, wi_wo
                     start=True,
                     stop=True,
                 )
+            return sums
+
+        def emit(first, width, empty_on, sums):
+            cols = slice(first, first + width)
             for c in range(OUT_TILES):
                 if empty_on[c] == "s":
                     nc.scalar.activation(result[:, c, cols], sums[c], ACT.Identity, bias=bias[:, c : c + 1])
@@ -176,44 +164,43 @@ def tile_list_net_drive_trials_kernel(tc, tab_words, tab_scales, offs, we, wi_wo
             nc.sync.dma_start(out_rows[:, :, cols], result[:, :, cols])
 
         nc.vector.memset(tab_sc[:], 0)
+        nc.vector.memset(v_sc_early[:].rearrange("p a s -> p (a s)").bitcast(I32), 0)
+        nc.vector.memset(v_sc_last[:].bitcast(I32), 0)
         nc.vector.memset(wi_sc_raw[:], 0)
-        nc.vector.memset(v_sc_low[:].rearrange("p a s -> p (a s)").bitcast(I32), 0)
         nc.sync.dma_start(offsets[:], offs)
-        load_tab(0, "tab0")
-        load_we(0, "we_raw0")
+        nc.sync.dma_start(wi_raw[:], wi_words.bitcast(I32).rearrange("a p c -> p a c"))
+        nc.sync.dma_start(tab_sc[0:P:4, :], tab_scales[0:2].bitcast(I32).rearrange("a j c -> j a c"))
+        nc.sync.dma_start(tab_sc[2:P:8, :], tab_scales[2].bitcast(I32))
+        for r in range(4):
+            nc.scalar.dma_start(
+                wi_sc_raw[r:P:32, :, :],
+                wi_scales.bitcast(I32).rearrange("a (q r) c -> r q a c", r=4)[r],
+            )
+        load_tab(0)
+        load_tab(1)
+
+        nc.vector.tensor_copy(picked_sc[:], tab_sc[:].bitcast(U8).indirect(picks(0, S)))
         for q in range(4):
             nc.sync.dma_start(
-                tab_sc[32 * q : 32 * q + 4 * PASSES, :], tab_scales[:, 4 * q : 4 * q + 4, :].bitcast(I32)
+                v_sc_early[32 * q : 32 * q + 4, :, :].bitcast(I32), picked_sc[32 * q : 32 * q + 32 : 4, :].bitcast(I32)
             )
-        for r in range(2):
+        load_we(0)
+        for q in range(4):
             nc.sync.dma_start(
-                wi_sc_raw[r:P:32, :, :],
-                wi_scales.bitcast(I32).rearrange("a (q r) c -> r q a c", r=4)[r],
+                v_sc_last[32 * q : 32 * q + 4, :].bitcast(I32), picked_sc[32 * q + 2 : 32 * q + 32 : 8, :].bitcast(I32)
             )
-        load_tab(1, "slot_c")
-        for r in range(2, 4):
-            nc.sync.dma_start(
-                wi_sc_raw[r:P:32, :, :],
-                wi_scales.bitcast(I32).rearrange("a (q r) c -> r q a c", r=4)[r],
-            )
-        nc.sync.dma_start(wi_raw[:], wi_words.bitcast(I32).rearrange("a p c -> p a c"))
-        load_we(1, "slot_d")
-        load_tab(2, "slot_a")
-        load_we(2, "slot_b")
-
-        gather_words(0, 0, S)
-        nc.vector.tensor_copy(v_sc[:], tab_sc[:].bitcast(U8).indirect(picks(0, S)))
-        for a in range(1, PASSES):
-            nc.scalar.dma_start(
-                v_sc_low[0:112, a - 1, :].bitcast(I32), v_sc[4 * a : 4 * a + 112, :].bitcast(I32)
-            )
-        we_bf[0] = sbuf("we_bf0", [P, SLOTS * H], BF16)
+        load_tab(2)
+        load_we(1)
+        load_we(2)
+        load_gain(0)
         for t in range(SLOTS):
-            round_we(0, t, we_bf[0][:, H * t : H * (t + 1)], False)
-        quantize_we(0, 0, H, we_bf[0][:])
-        for t in range(SLOTS):
-            excite(t, 0, 0)
-
+            nc.sync.dma_start(wo_raw[:, t, :], wo_rows[t])
+        load_gain(1)
+        load_gain(2)
+        load_gain(3)
+        with nc.allow_non_contiguous_dma(reason="one bias value for each partition and output tile"):
+            nc.sync.dma_start(bias[:], bo.rearrange("(c p) -> p c", p=P))
+        wi_codes = sbuf("wi_codes", [P, SLOTS, PASSES, 2 * P], U8, "slot_sc")
         nc.vector.tensor_copy(
             wi_codes[:].rearrange("p t a c -> p t (a c)").bitcast(I32).rearrange("p t (u e) -> p t u e", e=2),
             wi_raw[:].rearrange("p a (w t e) -> p t (a w) e", t=SLOTS, e=2),
@@ -223,61 +210,66 @@ def tile_list_net_drive_trials_kernel(tc, tab_words, tab_scales, offs, we, wi_wo
             wi_sc_raw[:].rearrange("p a (w t) -> p t (a w)", t=SLOTS),
         )
 
-        gather_words(1, 0, S)
-        load_gain(0, "slot_c")
+        gather_words(0, 0, HALF)
+        gather_words(0, HALF, HALF)
         for t in range(SLOTS):
             inhibit(t, 0, 0)
-        we_bf[1] = sbuf("we_bf1", [P, SLOTS * H], BF16, "slot_g")
+        gather_words(1, 0, S)
         for t in range(SLOTS):
-            round_we(1, t, we_bf[1][:, H * t : H * (t + 1)], t >= 2)
-        wo_raw = sbuf("wo_raw", [P, SLOTS, N], F32, "slot_d")
+            inhibit(t, 0, 1)
+        we_bf0 = [sbuf(f"we_bf0_{u}", [P, 2 * H], BF16) for u in range(2)]
+        round_we(0, 0, 2, we_bf0[0][:], False)
+        round_we(0, 2, 2, we_bf0[1][:], True)
+        for u in range(2):
+            quantize_we(0, 2 * u, 2, we_bf0[u][:])
         for t in range(SLOTS):
-            nc.sync.dma_start(wo_raw[:, t, :], wo_rows[t])
-        quantize_we(1, 0, H, we_bf[1][:])
+            excite(t, 0, 0)
 
         gather_words(2, 0, HALF)
         gather_words(2, HALF, HALF)
-        load_gain(1, "slot_a")
-        early = [c for c in CHUNKS if c[0] < HALF]
-        late = [c for c in CHUNKS if c[0] >= HALF]
-        h_early = sbuf("h_early", [P, SLOTS, HALF], F32)
-        diff_early = [sbuf(f"diff_early{t}", [P, HALF], F32) for t in range(SLOTS - 1)]
-        diff_last = [sbuf(f"diff_last{k}", [P, c[1]], F32, f"slot_last{k}") for k, c in enumerate(early)]
         for t in range(SLOTS):
-            for a in range(1, PASSES):
-                inhibit(t, 0, a)
+            inhibit(t, 0, 2)
+        rectify_i(0, 0)
+        rectify_i(1, 0)
+        we_bf1 = [sbuf(f"we_bf1_{u}", [P, 2 * H], BF16) for u in range(2)]
+        for u in range(2):
+            round_we(1, 2 * u, 2, we_bf1[u][:], True)
+        for u in range(2):
+            quantize_we(1, 2 * u, 2, we_bf1[u][:])
         for t in range(SLOTS):
             excite(t, 0, 1)
-        for t in range(SLOTS):
-            rounded = sbuf(f"we_bf2_{t}", [P, H], BF16, f"slot_r{t}")
-            round_we(2, t, rounded[:], t < SLOTS - 1)
-            quantize_we(2, P * t, P, rounded[:])
-            if t == 0:
-                load_gain(2, "slot_r0")
-            excite(t, 0, 2)
-            rectify_i(t, 0, f"slot_r{t}" if t > 0 else None)
-            if t < SLOTS - 1:
-                subtract(t, 0, HALF, diff_early[t][:])
-                apply_gain(t, 0, HALF, h_early[:, t, :], diff_early[t][:])
-            else:
-                for k, c in enumerate(early):
-                    subtract(t, c[0], c[1], diff_last[k][:])
-        load_gain(3, "slot_b")
-        bias = sbuf("bias", [P, OUT_TILES], F32, "diff_early0")
-        with nc.allow_non_contiguous_dma(reason="one bias value for each partition and output tile"):
-            nc.sync.dma_start(bias[:], bo.rearrange("(c p) -> p c", p=P))
 
-        def second_half_sums(t):
-            for a in pass_order[1]:
-                excite(t, 1, a)
+        we_bf2 = [sbuf(f"we_bf2_{t}", [P, H], BF16, f"slot_r{t}") for t in range(SLOTS)]
+        for t in range(SLOTS):
+            round_we(2, t, 1, we_bf2[t][:], t < 2)
+        for t in range(SLOTS):
+            quantize_we(2, t, 1, we_bf2[t][:])
+            excite(t, 0, 2)
+        rectify_i(2, 0, "slot_r2")
+        rectify_i(3, 0, "slot_r3")
+        last = SLOTS - 1
+        stage = sbuf("stage", [P, 2 + SLOTS, HALF], F32)
+        h_first = stage[:, 2:, :]
+        for t in range(last):
+            subtract(t, 0)
+            apply_gain(t, 0, HALF, h_first[:, t, :], diff[t, 0][:])
+        nc.vector.scalar_tensor_tensor(
+            stage[:, 0:2, 0:256],
+            e_bank[last][:].rearrange("p (u c) -> p u c", u=2),
+            0.0,
+            relu_i[last, 0][:].rearrange("p (u c) -> p u c", u=2),
+            ALU.max,
+            ALU.subtract,
+        )
+
+        for t in range(SLOTS):
             for a in range(PASSES):
                 inhibit(t, 1, a)
-            rectify_i(t, 1, None)
+            rectify_i(t, 1, "slot_r0" if t == 1 else None)
+            for a in range(PASSES):
+                excite(t, 1, a)
+            subtract(t, 1)
 
-        for t in range(SLOTS):
-            second_half_sums(t)
-
-        wo_bf = sbuf("wo_bf", [P, SLOTS * N], BF16)
         nc.scalar.activation(
             wo_bf[:].rearrange("p (c i t) -> p c t i", i=4, t=SLOTS),
             wo_raw[:].rearrange("p t (c i) -> p c t i", i=4),
@@ -290,36 +282,23 @@ def tile_list_net_drive_trials_kernel(tc, tab_words, tab_scales, offs, we, wi_wo
                 in_=wo_bf[:, 4 * first : 4 * (first + width)],
             )
 
-        n_free = 1
-        mid, tail = late[0], late[1:]
-        diff_free = sbuf("diff_free", [P, n_free, HALF], F32)
-        h_mid = sbuf("h_mid", [P, SLOTS, mid[1]], F32)
-        for t in range(n_free):
-            subtract(t, HALF, HALF, diff_free[:, t, :])
-            apply_gain(t, HALF, mid[1], h_mid[:, t, :], diff_free[:, t, : mid[1]])
-        for k, c in enumerate(early):
-            apply_gain(3, c[0], c[1], h_early[:, 3, c[0] : c[0] + c[1]], diff_last[k][:])
-        made = [quantize_h(c[0], c[1], c[2], h_early[:, :, c[0] : c[0] + c[1]]) for c in early]
-        diff_held = sbuf("diff_held", [P, SLOTS - n_free, HALF], F32, "slot_last0")
-        diff_late = [diff_free[:, t, :] if t < n_free else diff_held[:, t - n_free, :] for t in range(SLOTS)]
-        last = HALF - tail[-1][1]
-        for t in range(n_free, SLOTS):
-            subtract(t, HALF, last, diff_late[t][:, :last])
-        for t in range(n_free, SLOTS):
-            apply_gain(t, HALF, mid[1], h_mid[:, t, :], diff_late[t][:, : mid[1]])
-        emit(early[0][0], early[0][1], early[0][3], *made[0], e_bank[0:2])
-        made.append(quantize_h(mid[0], mid[1], mid[2], h_mid[:]))
-
-        def gains_and_codes(c, slot):
-            h_tail = sbuf(f"h_tail{c[0]}", [P, SLOTS, c[1]], F32, slot)
-            for t in range(SLOTS):
-                apply_gain(t, c[0], c[1], h_tail[:, t, :], diff_late[t][:, c[0] - HALF : c[0] - HALF + c[1]])
-            return quantize_h(c[0], c[1], c[2], h_tail[:])
-
-        made.append(gains_and_codes(tail[0], "h_bf0"))
-        emit(early[1][0], early[1][1], early[1][3], *made[1], e_bank[2:4])
-        emit(mid[0], mid[1], mid[3], *made[2], e_bank[0:2])
-        emit(tail[0][0], tail[0][1], tail[0][3], *made[3], i_bank[0:1])
-        for t in range(n_free, SLOTS):
-            subtract(t, tail[1][0], tail[1][1], diff_late[t][:, last:])
-        emit(tail[1][0], tail[1][1], tail[1][3], *gains_and_codes(tail[1], "h_mid"), i_bank[1:4])
+        third = stage[:, 0:SLOTS, 0:256]
+        fourth = stage[:].rearrange("p r c -> p (r c)")[:, 1536:2560].rearrange("p (t c) -> p t c", t=SLOTS)
+        for u in range(2):
+            apply_gain(last, 256 * u, 256, h_first[:, last, 256 * u : 256 * (u + 1)], stage[:, u, 0:256])
+        rounded = [round_h(256 * u, 256, False, h_first[:, :, 256 * u : 256 * (u + 1)]) for u in range(2)]
+        sums0 = product(0, 0, 256, rounded[0])
+        sums1 = product(1, 256, 256, rounded[1])
+        for t in range(SLOTS):
+            apply_gain(t, 512, 256, third[:, t, :], diff[t, 1][:, 0:256])
+        emit(0, 256, "sss", sums0)
+        rounded.append(round_h(512, 256, False, third))
+        emit(256, 256, "sss", sums1)
+        sums2 = product(2, 512, 256, rounded[2])
+        for t in (1, 2, 3, 0):
+            apply_gain(t, 768, 256, fourth[:, t, :], diff[t, 1][:, 256:512])
+        emit(512, 256, "sss", sums2)
+        ends = [round_h(768 + 128 * u, 128, True, fourth[:, :, 128 * u : 128 * (u + 1)]) for u in range(2)]
+        sums = [product(3 + u, 768 + 128 * u, 128, ends[u]) for u in range(2)]
+        emit(768, 128, "svs", sums[0])
+        emit(896, 128, "vsv", sums[1])

@@ -22,6 +22,7 @@ SLOTS = 4
 HALF = 512
 OUT_TILES = N // P
 BANKS = 8
+LATE = 2
 
 
 def tile_list_net_drive_trials_kernel(tc, tab_words, tab_scales, offs, we, wi_words, wi_scales, gT, wo, bo, out):
@@ -45,7 +46,6 @@ def tile_list_net_drive_trials_kernel(tc, tab_words, tab_scales, offs, we, wi_wo
         wi_sc_raw = sbuf("wi_sc_raw", [P, PASSES, H // 4], I32)
         wi_sc = sbuf("wi_sc", [P, SLOTS, PASSES, P], U8)
         wo_raw = sbuf("wo_raw", [P, SLOTS, N], F32)
-        wo_bf = sbuf("wo_bf", [P, SLOTS * N], BF16)
         wo_codes = sbuf("wo_codes", [P, N], U32)
         wo_sc = sbuf("wo_sc", [P, N], U8)
         bias = sbuf("bias", [P, OUT_TILES], F32)
@@ -54,7 +54,12 @@ def tile_list_net_drive_trials_kernel(tc, tab_words, tab_scales, offs, we, wi_wo
         we_raw = [sbuf(f"we_raw{a}", [P, SLOTS, H], F32) for a in range(PASSES)]
         gain = [sbuf(f"gain{t}", [P, T], F32) for t in range(SLOTS)]
         banks = [psum.tile([P, HALF], F32, name=f"bank{b}") for b in range(BANKS)]
-        i_bank, e_bank = banks[:SLOTS], banks[SLOTS:]
+        e_bank = {(t, half): banks[SLOTS * half + t] for t in range(SLOTS) for half in range(2)}
+        i_bank = dict(e_bank)
+        i_bank[LATE, 1] = banks[0]
+        e_bank[1, 1] = banks[1]
+        e_bank[2, 1] = banks[2]
+        stage = sbuf("stage", [P, 2 + SLOTS, HALF], F32)
         v_words, relu_i, diff = {}, {}, {}
 
         gain_rows = gT.rearrange("(w t b) c -> t w b c", t=SLOTS, b=4)
@@ -94,7 +99,7 @@ def tile_list_net_drive_trials_kernel(tc, tab_words, tab_scales, offs, we, wi_wo
 
         def excite(t, half, a):
             nc.tensor.matmul_mx(
-                out=e_bank[t][:],
+                out=e_bank[t, half][:],
                 lhsT=we_codes[a][:, P * t : P * (t + 1)].bitcast(FP8X4),
                 lhsT_scale=we_sc[a][:, P * t : P * (t + 1)],
                 rhs=v_words[a, half].bitcast(FP8X4),
@@ -105,7 +110,7 @@ def tile_list_net_drive_trials_kernel(tc, tab_words, tab_scales, offs, we, wi_wo
 
         def inhibit(t, half, a):
             nc.tensor.matmul_mx(
-                out=i_bank[t][:],
+                out=i_bank[t, half][:],
                 lhsT=wi_codes[:, t, a, :].bitcast(FP4X4),
                 lhsT_scale=wi_sc[:, t, a, :],
                 rhs=v_words[a, half].bitcast(FP8X4),
@@ -114,15 +119,19 @@ def tile_list_net_drive_trials_kernel(tc, tab_words, tab_scales, offs, we, wi_wo
                 stop=(a == PASSES - 1),
             )
 
-        def rectify_i(t, half, slot=None):
-            relu_i[t, half] = sbuf(f"relu_i{t}_{half}", [P, HALF], F32, slot)
-            nc.scalar.activation(relu_i[t, half][:], i_bank[t][:], ACT.Relu)
+        def rectify_i(t, half, dst):
+            relu_i[t, half] = dst
+            nc.scalar.activation(dst, i_bank[t, half][:], ACT.Relu)
 
         def subtract(t, half):
-            diff[t, half] = sbuf(f"diff{t}_{half}", [P, HALF], F32)
             nc.vector.scalar_tensor_tensor(
-                diff[t, half][:], e_bank[t][:], 0.0, relu_i[t, half][:], ALU.max, ALU.subtract
+                diff[t, half], e_bank[t, half][:], 0.0, relu_i[t, half], ALU.max, ALU.subtract
             )
+
+        def subtract_beside(t, half, slot):
+            relu_e = sbuf(f"relu_e{t}_{half}", [P, HALF], F32, slot)
+            nc.scalar.activation(relu_e[:], e_bank[t, half][:], ACT.Relu)
+            nc.gpsimd.tensor_tensor(diff[t, half], relu_e[:], relu_i[t, half], ALU.subtract)
 
         def apply_gain(t, first, width, dst, src):
             nc.vector.tensor_tensor(dst, gain[t][:].indirect(picks(first, width)), src, ALU.mult)
@@ -154,14 +163,17 @@ def tile_list_net_drive_trials_kernel(tc, tab_words, tab_scales, offs, we, wi_wo
                 )
             return sums
 
-        def emit(first, width, empty_on, sums):
+        def emit(first, width, empty_on, sums, by_tile):
             cols = slice(first, first + width)
             for c in range(OUT_TILES):
                 if empty_on[c] == "s":
                     nc.scalar.activation(result[:, c, cols], sums[c], ACT.Identity, bias=bias[:, c : c + 1])
                 else:
                     nc.vector.tensor_scalar(result[:, c, cols], sums[c], bias[:, c : c + 1], None, ALU.add)
-            nc.sync.dma_start(out_rows[:, :, cols], result[:, :, cols])
+                if by_tile:
+                    nc.sync.dma_start(out_rows[:, c, cols], result[:, c, cols])
+            if not by_tile:
+                nc.sync.dma_start(out_rows[:, :, cols], result[:, :, cols])
 
         nc.vector.memset(tab_sc[:], 0)
         nc.vector.memset(v_sc_early[:].rearrange("p a s -> p (a s)").bitcast(I32), 0)
@@ -184,18 +196,18 @@ def tile_list_net_drive_trials_kernel(tc, tab_words, tab_scales, offs, we, wi_wo
             nc.sync.dma_start(
                 v_sc_early[32 * q : 32 * q + 4, :, :].bitcast(I32), picked_sc[32 * q : 32 * q + 32 : 4, :].bitcast(I32)
             )
+        load_tab(2)
         load_we(0)
         for q in range(4):
             nc.sync.dma_start(
                 v_sc_last[32 * q : 32 * q + 4, :].bitcast(I32), picked_sc[32 * q + 2 : 32 * q + 32 : 8, :].bitcast(I32)
             )
-        load_tab(2)
         load_we(1)
         load_we(2)
         load_gain(0)
+        load_gain(1)
         for t in range(SLOTS):
             nc.sync.dma_start(wo_raw[:, t, :], wo_rows[t])
-        load_gain(1)
         load_gain(2)
         load_gain(3)
         with nc.allow_non_contiguous_dma(reason="one bias value for each partition and output tile"):
@@ -212,64 +224,61 @@ def tile_list_net_drive_trials_kernel(tc, tab_words, tab_scales, offs, we, wi_wo
 
         gather_words(0, 0, HALF)
         gather_words(0, HALF, HALF)
-        for t in range(SLOTS):
-            inhibit(t, 0, 0)
         gather_words(1, 0, S)
-        for t in range(SLOTS):
-            inhibit(t, 0, 1)
-        we_bf0 = [sbuf(f"we_bf0_{u}", [P, 2 * H], BF16) for u in range(2)]
-        round_we(0, 0, 2, we_bf0[0][:], False)
-        round_we(0, 2, 2, we_bf0[1][:], True)
-        for u in range(2):
-            quantize_we(0, 2 * u, 2, we_bf0[u][:])
-        for t in range(SLOTS):
-            excite(t, 0, 0)
-
         gather_words(2, 0, HALF)
         gather_words(2, HALF, HALF)
-        for t in range(SLOTS):
-            inhibit(t, 0, 2)
-        rectify_i(0, 0)
-        rectify_i(1, 0)
-        we_bf1 = [sbuf(f"we_bf1_{u}", [P, 2 * H], BF16) for u in range(2)]
-        for u in range(2):
-            round_we(1, 2 * u, 2, we_bf1[u][:], True)
-        for u in range(2):
-            quantize_we(1, 2 * u, 2, we_bf1[u][:])
-        for t in range(SLOTS):
-            excite(t, 0, 1)
+        for a in range(PASSES):
+            for half in range(2):
+                for t in range(SLOTS):
+                    if (t, half) != (LATE, 1):
+                        inhibit(t, half, a)
 
+        for a in range(2):
+            we_bf = [sbuf(f"we_bf{a}_{u}", [P, 2 * H], BF16) for u in range(2)]
+            for u in range(2):
+                round_we(a, 2 * u, 2, we_bf[u][:], a == 1 or u == 0)
+            for u in range(2):
+                quantize_we(a, 2 * u, 2, we_bf[u][:])
+            if a == 0:
+                for t in range(SLOTS):
+                    rectify_i(t, 0, sbuf(f"relu_i{t}_0", [P, HALF], F32)[:])
+                rectify_i(1, 1, stage[:, 0, :])
+            for t in range(SLOTS):
+                excite(t, 0, a)
         we_bf2 = [sbuf(f"we_bf2_{t}", [P, H], BF16, f"slot_r{t}") for t in range(SLOTS)]
         for t in range(SLOTS):
             round_we(2, t, 1, we_bf2[t][:], t < 2)
         for t in range(SLOTS):
             quantize_we(2, t, 1, we_bf2[t][:])
             excite(t, 0, 2)
-        rectify_i(2, 0, "slot_r2")
-        rectify_i(3, 0, "slot_r3")
-        last = SLOTS - 1
-        stage = sbuf("stage", [P, 2 + SLOTS, HALF], F32)
-        h_first = stage[:, 2:, :]
-        for t in range(last):
-            subtract(t, 0)
-            apply_gain(t, 0, HALF, h_first[:, t, :], diff[t, 0][:])
-        nc.vector.scalar_tensor_tensor(
-            stage[:, 0:2, 0:256],
-            e_bank[last][:].rearrange("p (u c) -> p u c", u=2),
-            0.0,
-            relu_i[last, 0][:].rearrange("p (u c) -> p u c", u=2),
-            ALU.max,
-            ALU.subtract,
-        )
 
+        last = SLOTS - 1
+        flat = stage[:].rearrange("p r c -> p (r c)")
+        h_first = stage[:, 2:, :]
+        third = flat[:, 0:1024].rearrange("p (t c) -> p t c", t=SLOTS)
+        fourth = flat[:, 768:1792].rearrange("p (t c) -> p t c", t=SLOTS)
         for t in range(SLOTS):
-            for a in range(PASSES):
-                inhibit(t, 1, a)
-            rectify_i(t, 1, "slot_r0" if t == 1 else None)
+            diff[t, 0] = sbuf(f"diff{t}_0", [P, HALF], F32)[:] if t < last else stage[:, 1, :]
+            subtract(t, 0)
+            if t < last:
+                apply_gain(t, 0, HALF, h_first[:, t, :], diff[t, 0])
+
+        for k, t in enumerate((0, 3)):
+            rectify_i(t, 1, sbuf(f"relu_i{t}_1", [P, HALF], F32, f"slot_r{k}")[:])
+        for t in (0, 3, 2, 1):
+            diff[t, 1] = sbuf(f"diff{t}_1", [P, HALF], F32, "diff1_0" if t == 1 else None)[:]
+            if t == last:
+                for a in range(PASSES):
+                    inhibit(LATE, 1, a)
+                rectify_i(LATE, 1, sbuf("relu_i_late", [P, HALF], F32)[:])
             for a in range(PASSES):
                 excite(t, 1, a)
-            subtract(t, 1)
+            if t in (0, 3):
+                subtract_beside(t, 1, "relu_i3_0" if t == 3 else None)
+            else:
+                subtract(t, 1)
 
+        wo_bf = sbuf("wo_bf", [P, SLOTS * N], BF16)
         nc.scalar.activation(
             wo_bf[:].rearrange("p (c i t) -> p c t i", i=4, t=SLOTS),
             wo_raw[:].rearrange("p t (c i) -> p c t i", i=4),
@@ -282,23 +291,26 @@ def tile_list_net_drive_trials_kernel(tc, tab_words, tab_scales, offs, we, wi_wo
                 in_=wo_bf[:, 4 * first : 4 * (first + width)],
             )
 
-        third = stage[:, 0:SLOTS, 0:256]
-        fourth = stage[:].rearrange("p r c -> p (r c)")[:, 1536:2560].rearrange("p (t c) -> p t c", t=SLOTS)
         for u in range(2):
-            apply_gain(last, 256 * u, 256, h_first[:, last, 256 * u : 256 * (u + 1)], stage[:, u, 0:256])
+            cols = slice(256 * u, 256 * (u + 1))
+            apply_gain(last, 256 * u, 256, h_first[:, last, cols], diff[last, 0][:, cols])
         rounded = [round_h(256 * u, 256, False, h_first[:, :, 256 * u : 256 * (u + 1)]) for u in range(2)]
         sums0 = product(0, 0, 256, rounded[0])
         sums1 = product(1, 256, 256, rounded[1])
         for t in range(SLOTS):
             apply_gain(t, 512, 256, third[:, t, :], diff[t, 1][:, 0:256])
-        emit(0, 256, "sss", sums0)
         rounded.append(round_h(512, 256, False, third))
-        emit(256, 256, "sss", sums1)
+        emit(0, 256, "sss", sums0, True)
+        emit(256, 256, "sss", sums1, True)
         sums2 = product(2, 512, 256, rounded[2])
-        for t in (1, 2, 3, 0):
+        for t in (1, 3, 2):
             apply_gain(t, 768, 256, fourth[:, t, :], diff[t, 1][:, 256:512])
-        emit(512, 256, "sss", sums2)
+        for u in range(2):
+            apply_gain(
+                0, 768 + 128 * u, 128, fourth[:, 0, 128 * u : 128 * (u + 1)], diff[0, 1][:, 256 + 128 * u : 384 + 128 * u]
+            )
+        emit(512, 256, "sss", sums2, True)
         ends = [round_h(768 + 128 * u, 128, True, fourth[:, :, 128 * u : 128 * (u + 1)]) for u in range(2)]
         sums = [product(3 + u, 768 + 128 * u, 128, ends[u]) for u in range(2)]
-        emit(768, 128, "svs", sums[0])
-        emit(896, 128, "vsv", sums[1])
+        emit(768, 128, "svs", sums[0], False)
+        emit(896, 128, "vsv", sums[1], False)

@@ -40,8 +40,6 @@ def tile_list_net_drive_trials_kernel(tc, tab_words, tab_scales, offs, we, wi_wo
         v_sc_early = sbuf("v_sc_early", [P, 2, S], U8)
         v_sc_last = sbuf("v_sc_last", [P, S], U8)
         v_sc = [v_sc_early[:, 0, :], v_sc_early[:, 1, :], v_sc_last[:]]
-        we_codes = [sbuf(f"we_codes{a}", [P, H], U32) for a in range(PASSES)]
-        we_sc = [sbuf(f"we_sc{a}", [P, H], U8) for a in range(PASSES)]
         wi_raw = sbuf("wi_raw", [P, PASSES, 2 * H // 4], I32)
         wi_sc_raw = sbuf("wi_sc_raw", [P, PASSES, H // 4], I32)
         wi_sc = sbuf("wi_sc", [P, SLOTS, PASSES, P], U8)
@@ -57,10 +55,11 @@ def tile_list_net_drive_trials_kernel(tc, tab_words, tab_scales, offs, we, wi_wo
         e_bank = {(t, half): banks[SLOTS * half + t] for t in range(SLOTS) for half in range(2)}
         i_bank = dict(e_bank)
         i_bank[LATE, 1] = banks[0]
+        e_bank[0, 1] = banks[SLOTS + LATE]
         e_bank[1, 1] = banks[1]
         e_bank[2, 1] = banks[2]
         stage = sbuf("stage", [P, 2 + SLOTS, HALF], F32)
-        v_words, relu_i, diff = {}, {}, {}
+        v_words, we_codes, we_sc, relu_i, diff = {}, {}, {}, {}, {}
 
         gain_rows = gT.rearrange("(w t b) c -> t w b c", t=SLOTS, b=4)
         wo_rows = wo.rearrange("(w t b) n -> t w b n", t=SLOTS, b=4)
@@ -93,15 +92,19 @@ def tile_list_net_drive_trials_kernel(tc, tab_words, tab_scales, offs, we, wi_wo
                 for u in range(count):
                     nc.scalar.activation(dst[:, u], src[:, u], ACT.Copy)
 
-        def quantize_we(a, t, count, rounded):
-            cols = slice(P * t, P * (t + count))
-            nc.vector.quantize_mx(out=we_codes[a][:, cols].bitcast(FP8X4), scales=we_sc[a][:, cols], in_=rounded)
+        def quantize_we(a, t, count, rounded, slot=None):
+            codes = sbuf(f"we_codes{a}_{t}", [P, P * count], U32, slot)
+            scales = sbuf(f"we_sc{a}_{t}", [P, P * count], U8)
+            nc.vector.quantize_mx(out=codes[:].bitcast(FP8X4), scales=scales[:], in_=rounded)
+            for u in range(count):
+                we_codes[a, t + u] = codes[:, P * u : P * (u + 1)]
+                we_sc[a, t + u] = scales[:, P * u : P * (u + 1)]
 
         def excite(t, half, a):
             nc.tensor.matmul_mx(
                 out=e_bank[t, half][:],
-                lhsT=we_codes[a][:, P * t : P * (t + 1)].bitcast(FP8X4),
-                lhsT_scale=we_sc[a][:, P * t : P * (t + 1)],
+                lhsT=we_codes[a, t].bitcast(FP8X4),
+                lhsT_scale=we_sc[a, t],
                 rhs=v_words[a, half].bitcast(FP8X4),
                 rhs_scale=v_sc[a][:, HALF * half : HALF * (half + 1)],
                 start=(a == 0),
@@ -172,8 +175,6 @@ def tile_list_net_drive_trials_kernel(tc, tab_words, tab_scales, offs, we, wi_wo
                     nc.vector.tensor_scalar(result[:, c, cols], sums[c], bias[:, c : c + 1], None, ALU.add)
                 if by_tile:
                     nc.sync.dma_start(out_rows[:, c, cols], result[:, c, cols])
-            if not by_tile:
-                nc.sync.dma_start(out_rows[:, :, cols], result[:, :, cols])
 
         nc.vector.memset(tab_sc[:], 0)
         nc.vector.memset(v_sc_early[:].rearrange("p a s -> p (a s)").bitcast(I32), 0)
@@ -233,24 +234,30 @@ def tile_list_net_drive_trials_kernel(tc, tab_words, tab_scales, offs, we, wi_wo
                     if (t, half) != (LATE, 1):
                         inhibit(t, half, a)
 
-        for a in range(2):
-            we_bf = [sbuf(f"we_bf{a}_{u}", [P, 2 * H], BF16) for u in range(2)]
-            for u in range(2):
-                round_we(a, 2 * u, 2, we_bf[u][:], a == 1 or u == 0)
-            for u in range(2):
-                quantize_we(a, 2 * u, 2, we_bf[u][:])
-            if a == 0:
-                for t in range(SLOTS):
-                    rectify_i(t, 0, sbuf(f"relu_i{t}_0", [P, HALF], F32)[:])
-                rectify_i(1, 1, stage[:, 0, :])
-            for t in range(SLOTS):
-                excite(t, 0, a)
+        we_bf = [[sbuf(f"we_bf{a}_{u}", [P, 2 * H], BF16) for u in range(2)] for a in range(2)]
+        for u in range(2):
+            round_we(0, 2 * u, 2, we_bf[0][u][:], u == 1)
+        for u in range(2):
+            quantize_we(0, 2 * u, 2, we_bf[0][u][:])
+        for t in range(SLOTS):
+            rectify_i(t, 0, sbuf(f"relu_i{t}_0", [P, HALF], F32)[:])
+        rectify_i(1, 1, stage[:, 0, :])
+        for t in range(SLOTS):
+            excite(t, 0, 0)
+        for u in range(2):
+            round_we(1, 2 * u, 2, we_bf[1][u][:], True)
+        quantize_we(1, 0, 2, we_bf[1][0][:])
+        for t in range(2):
+            excite(t, 0, 1)
         we_bf2 = [sbuf(f"we_bf2_{t}", [P, H], BF16, f"slot_r{t}") for t in range(SLOTS)]
         for t in range(SLOTS):
             round_we(2, t, 1, we_bf2[t][:], t < 2)
         for t in range(SLOTS):
             quantize_we(2, t, 1, we_bf2[t][:])
-            excite(t, 0, 2)
+        quantize_we(1, 2, 2, we_bf[1][1][:], "slot_r0")
+        for t in range(SLOTS):
+            for a in range(2 if t < 2 else 1, PASSES):
+                excite(t, 0, a)
 
         last = SLOTS - 1
         flat = stage[:].rearrange("p r c -> p (r c)")
@@ -264,7 +271,7 @@ def tile_list_net_drive_trials_kernel(tc, tab_words, tab_scales, offs, we, wi_wo
                 apply_gain(t, 0, HALF, h_first[:, t, :], diff[t, 0])
 
         for k, t in enumerate((0, 3)):
-            rectify_i(t, 1, sbuf(f"relu_i{t}_1", [P, HALF], F32, f"slot_r{k}")[:])
+            rectify_i(t, 1, sbuf(f"relu_i{t}_1", [P, HALF], F32, f"slot_r{k + 1}")[:])
         for t in (0, 3, 2, 1):
             diff[t, 1] = sbuf(f"diff{t}_1", [P, HALF], F32, "diff1_0" if t == 1 else None)[:]
             if t == last:
@@ -274,7 +281,7 @@ def tile_list_net_drive_trials_kernel(tc, tab_words, tab_scales, offs, we, wi_wo
             for a in range(PASSES):
                 excite(t, 1, a)
             if t in (0, 3):
-                subtract_beside(t, 1, "relu_i3_0" if t == 3 else None)
+                subtract_beside(t, 1, "relu_i3_0" if t == 3 else "relu_i1_0")
             else:
                 subtract(t, 1)
 
@@ -314,3 +321,5 @@ def tile_list_net_drive_trials_kernel(tc, tab_words, tab_scales, offs, we, wi_wo
         sums = [product(3 + u, 768 + 128 * u, 128, ends[u]) for u in range(2)]
         emit(768, 128, "svs", sums[0], False)
         emit(896, 128, "vsv", sums[1], False)
+        for c in range(OUT_TILES):
+            nc.sync.dma_start(out_rows[:, c, 768:S], result[:, c, 768:S])

@@ -23,6 +23,7 @@ HALF = 512
 OUT_TILES = N // P
 BANKS = 8
 LATE = 2
+QUADRANTS = (0, 2, 1, 3)
 
 
 def tile_list_net_drive_trials_kernel(tc, tab_words, tab_scales, offs, we, wi_words, wi_scales, gT, wo, bo, out):
@@ -183,7 +184,7 @@ def tile_list_net_drive_trials_kernel(tc, tab_words, tab_scales, offs, we, wi_wo
         nc.sync.dma_start(offsets[:], offs)
         nc.sync.dma_start(wi_raw[:], wi_words.bitcast(I32).rearrange("a p c -> p a c"))
         nc.sync.dma_start(tab_sc[0:P:4, :], tab_scales[0:2].bitcast(I32).rearrange("a j c -> j a c"))
-        nc.sync.dma_start(tab_sc[2:P:8, :], tab_scales[2].bitcast(I32))
+        nc.sync.dma_start(tab_sc[6:P:8, :], tab_scales[2].bitcast(I32))
         for r in range(4):
             nc.scalar.dma_start(
                 wi_sc_raw[r:P:32, :, :],
@@ -193,15 +194,15 @@ def tile_list_net_drive_trials_kernel(tc, tab_words, tab_scales, offs, we, wi_wo
         load_tab(1)
 
         nc.vector.tensor_copy(picked_sc[:], tab_sc[:].bitcast(U8).indirect(picks(0, S)))
-        for q in range(4):
+        for q in QUADRANTS:
             nc.sync.dma_start(
                 v_sc_early[32 * q : 32 * q + 4, :, :].bitcast(I32), picked_sc[32 * q : 32 * q + 32 : 4, :].bitcast(I32)
             )
         load_tab(2)
         load_we(0)
-        for q in range(4):
+        for q in QUADRANTS:
             nc.sync.dma_start(
-                v_sc_last[32 * q : 32 * q + 4, :].bitcast(I32), picked_sc[32 * q + 2 : 32 * q + 32 : 8, :].bitcast(I32)
+                v_sc_last[32 * q : 32 * q + 4, :].bitcast(I32), picked_sc[32 * q + 6 : 32 * q + 32 : 8, :].bitcast(I32)
             )
         load_we(1)
         load_we(2)

@@ -22,8 +22,11 @@ SLOTS = 4
 HALF = 512
 OUT_TILES = N // P
 BANKS = 8
-LATE = 2
+CHUNK = 256
 QUADRANTS = (0, 2, 1, 3)
+WARM = 3
+TAB2_CUT = 512
+LATE = (2, 1)
 
 
 def tile_list_net_drive_trials_kernel(tc, tab_words, tab_scales, offs, we, wi_words, wi_scales, gT, wo, bo, out):
@@ -53,13 +56,15 @@ def tile_list_net_drive_trials_kernel(tc, tab_words, tab_scales, offs, we, wi_wo
         we_raw = [sbuf(f"we_raw{a}", [P, SLOTS, H], F32) for a in range(PASSES)]
         gain = [sbuf(f"gain{t}", [P, T], F32) for t in range(SLOTS)]
         banks = [psum.tile([P, HALF], F32, name=f"bank{b}") for b in range(BANKS)]
-        e_bank = {(t, half): banks[SLOTS * half + t] for t in range(SLOTS) for half in range(2)}
-        i_bank = dict(e_bank)
-        i_bank[LATE, 1] = banks[0]
-        e_bank[0, 1] = banks[SLOTS + LATE]
-        e_bank[1, 1] = banks[1]
-        e_bank[2, 1] = banks[2]
-        stage = sbuf("stage", [P, 2 + SLOTS, HALF], F32)
+        bank = {(t, half): banks[SLOTS * half + t] for t in range(SLOTS) for half in range(2)}
+        stage = sbuf("stage", [P, SLOTS + 2, HALF], F32)
+        flat = stage[:].rearrange("p u c -> p (u c)")
+        third = flat[:, 0:1024].rearrange("p (t c) -> p t c", t=SLOTS)
+        fourth = flat[:, 768:1792].rearrange("p (t c) -> p t c", t=SLOTS)
+        shared = sbuf("shared", [P, 5, CHUNK], F32)
+        h_bf = {first: sbuf(f"h_bf{first}", [P, SLOTS * CHUNK], BF16)[:] for first in (0, CHUNK, 2 * CHUNK)}
+        for first in (3 * CHUNK, 3 * CHUNK + P):
+            h_bf[first] = sbuf(f"h_bf{first}", [P, SLOTS * P], BF16)[:]
         v_words, we_codes, we_sc, relu_i, diff = {}, {}, {}, {}, {}
 
         gain_rows = gT.rearrange("(w t b) c -> t w b c", t=SLOTS, b=4)
@@ -69,8 +74,9 @@ def tile_list_net_drive_trials_kernel(tc, tab_words, tab_scales, offs, we, wi_wo
         def picks(first, width):
             return offsets[:, first // 16 : (first + width) // 16]
 
-        def load_tab(a):
-            nc.sync.dma_start(tab[a][:], tab_words[a].rearrange("p t i -> p (t i)").bitcast(I32))
+        def load_tab(a, first=0, last=T):
+            words = tab_words[a].rearrange("p t i -> p (t i)").bitcast(I32)
+            nc.sync.dma_start(tab[a][:, first:last], words[:, first:last])
 
         def load_we(a):
             nc.sync.dma_start(we_raw[a][:], we[512 * a : 512 * (a + 1), :].rearrange("(p j) r -> p j r", j=4))
@@ -78,83 +84,99 @@ def tile_list_net_drive_trials_kernel(tc, tab_words, tab_scales, offs, we, wi_wo
         def load_gain(t):
             nc.sync.dma_start(gain[t][:], gain_rows[t])
 
-        def gather_words(a, first, width):
-            picked = sbuf(f"v_words{a}_{first}", [P, width], U32)
-            nc.vector.tensor_copy(picked[:], tab[a][:].bitcast(U32).indirect(picks(first, width)))
-            for half in range(first // HALF, (first + width) // HALF):
-                v_words[a, half] = picked[:, HALF * half - first : HALF * (half + 1) - first]
+        def gather_words(a, half, slot=None):
+            picked = sbuf(f"v_words{a}_{half}", [P, HALF], U32, slot)
+            nc.vector.tensor_copy(picked[:], tab[a][:].bitcast(U32).indirect(picks(HALF * half, HALF)))
+            v_words[a, half] = picked[:]
 
-        def round_we(a, t, count, rounded, on_vector):
-            dst = rounded.rearrange("p (t w b j) -> p t w j b", t=count, b=4, j=4)
+        def round_we(a, t, count, on_vector, slot=None):
+            rounded = sbuf(f"we_bf{a}_{t}", [P, count * H], BF16, slot)
+            dst = rounded[:].rearrange("p (t w b j) -> p t w j b", t=count, b=4, j=4)
             src = we_raw[a][:].rearrange("p j (w t b) -> p t w j b", t=SLOTS, b=4)[:, t : t + count]
             if on_vector:
                 nc.vector.tensor_copy(dst, src)
             else:
                 for u in range(count):
                     nc.scalar.activation(dst[:, u], src[:, u], ACT.Copy)
+            return rounded[:]
 
-        def quantize_we(a, t, count, rounded, slot=None):
-            codes = sbuf(f"we_codes{a}_{t}", [P, P * count], U32, slot)
+        def quantize_we(a, t, count, rounded):
+            codes = sbuf(f"we_codes{a}_{t}", [P, P * count], U32)
             scales = sbuf(f"we_sc{a}_{t}", [P, P * count], U8)
             nc.vector.quantize_mx(out=codes[:].bitcast(FP8X4), scales=scales[:], in_=rounded)
             for u in range(count):
                 we_codes[a, t + u] = codes[:, P * u : P * (u + 1)]
                 we_sc[a, t + u] = scales[:, P * u : P * (u + 1)]
 
-        def excite(t, half, a):
+        def excite(t, half, a, start, stop):
             nc.tensor.matmul_mx(
-                out=e_bank[t, half][:],
+                out=bank[t, half][:],
                 lhsT=we_codes[a, t].bitcast(FP8X4),
                 lhsT_scale=we_sc[a, t],
                 rhs=v_words[a, half].bitcast(FP8X4),
                 rhs_scale=v_sc[a][:, HALF * half : HALF * (half + 1)],
-                start=(a == 0),
-                stop=(a == PASSES - 1),
+                start=start,
+                stop=stop,
             )
 
-        def inhibit(t, half, a):
+        def inhibit(t, half, a, start, stop):
             nc.tensor.matmul_mx(
-                out=i_bank[t, half][:],
+                out=bank[t, half][:],
                 lhsT=wi_codes[:, t, a, :].bitcast(FP4X4),
                 lhsT_scale=wi_sc[:, t, a, :],
                 rhs=v_words[a, half].bitcast(FP8X4),
                 rhs_scale=v_sc[a][:, HALF * half : HALF * (half + 1)],
-                start=(a == 0),
-                stop=(a == PASSES - 1),
+                start=start,
+                stop=stop,
             )
 
         def rectify_i(t, half, dst):
             relu_i[t, half] = dst
-            nc.scalar.activation(dst, i_bank[t, half][:], ACT.Relu)
+            nc.scalar.activation(dst, bank[t, half][:], ACT.Relu)
 
-        def subtract(t, half):
+        def differences(t, half, cols):
+            if (t, half) == (3, 0) and cols.start:
+                return shared[:, 2, :]
+            return diff[t, half][:, cols]
+
+        def subtract(t, half, lo=0, width=HALF):
+            cols = slice(lo, lo + width)
             nc.vector.scalar_tensor_tensor(
-                diff[t, half], e_bank[t, half][:], 0.0, relu_i[t, half], ALU.max, ALU.subtract
+                differences(t, half, cols), bank[t, half][:, cols], 0.0, relu_i[t, half][:, cols], ALU.max, ALU.subtract
             )
 
-        def subtract_beside(t, half, slot):
-            relu_e = sbuf(f"relu_e{t}_{half}", [P, HALF], F32, slot)
-            nc.scalar.activation(relu_e[:], e_bank[t, half][:], ACT.Relu)
+        def subtract_beside(t, half):
+            relu_e = sbuf(f"relu_e{t}_{half}", [P, HALF], F32)
+            nc.scalar.activation(relu_e[:], bank[t, half][:], ACT.Relu)
             nc.gpsimd.tensor_tensor(diff[t, half], relu_e[:], relu_i[t, half], ALU.subtract)
 
-        def apply_gain(t, first, width, dst, src):
-            nc.vector.tensor_tensor(dst, gain[t][:].indirect(picks(first, width)), src, ALU.mult)
+        def h_cols(first, width):
+            chunk, lo = divmod(first, CHUNK)
+            if chunk < 2:
+                return stage[:, 2:, first : first + width]
+            return (third if chunk == 2 else fourth)[:, :, lo : lo + width]
 
-        def round_h(first, width, on_vector, h_f32):
-            h_bf = sbuf(f"h_bf{first}", [P, SLOTS * width], BF16)
-            h_dst = h_bf[:].rearrange("p (c i t) -> p c t i", i=4, t=SLOTS)
-            h_src = h_f32.rearrange("p t (c i) -> p c t i", i=4)
+        def apply_gain(t, first, width):
+            half, lo = divmod(first, HALF)
+            cols = slice(lo, lo + width)
+            nc.vector.tensor_tensor(
+                h_cols(first, width)[:, t, :], gain[t][:].indirect(picks(first, width)), differences(t, half, cols), ALU.mult
+            )
+
+        def round_h(first, lo, width, on_vector):
+            values = h_cols(first + lo, width)
+            h_dst = h_bf[first][:, SLOTS * lo : SLOTS * (lo + width)].rearrange("p (c i t) -> p c t i", i=4, t=SLOTS)
+            h_src = values.rearrange("p t (c i) -> p c t i", i=4)
             if on_vector:
                 nc.vector.tensor_copy(h_dst, h_src)
             else:
                 nc.scalar.activation(h_dst, h_src, ACT.Copy)
-            return h_bf
 
-        def product(chunk, first, width, h_bf):
+        def product(step, first, width):
             h_codes = sbuf(f"h_codes{first}", [P, width], U32)
             h_sc = sbuf(f"h_sc{first}", [P, width], U8)
-            nc.vector.quantize_mx(out=h_codes[:].bitcast(FP8X4), scales=h_sc[:], in_=h_bf[:])
-            sums = [banks[(OUT_TILES * chunk + c) % BANKS][:, :width] for c in range(OUT_TILES)]
+            nc.vector.quantize_mx(out=h_codes[:].bitcast(FP8X4), scales=h_sc[:], in_=h_bf[first])
+            sums = [banks[(OUT_TILES * step + c) % BANKS][:, :width] for c in range(OUT_TILES)]
             for c in range(OUT_TILES):
                 nc.tensor.matmul_mx(
                     out=sums[c],
@@ -192,13 +214,14 @@ def tile_list_net_drive_trials_kernel(tc, tab_words, tab_scales, offs, we, wi_wo
             )
         load_tab(0)
         load_tab(1)
+        load_tab(2, 0, TAB2_CUT)
 
         nc.vector.tensor_copy(picked_sc[:], tab_sc[:].bitcast(U8).indirect(picks(0, S)))
         for q in QUADRANTS:
             nc.sync.dma_start(
                 v_sc_early[32 * q : 32 * q + 4, :, :].bitcast(I32), picked_sc[32 * q : 32 * q + 32 : 4, :].bitcast(I32)
             )
-        load_tab(2)
+        load_tab(2, TAB2_CUT, T)
         load_we(0)
         for q in QUADRANTS:
             nc.sync.dma_start(
@@ -224,68 +247,89 @@ def tile_list_net_drive_trials_kernel(tc, tab_words, tab_scales, offs, we, wi_wo
             wi_sc_raw[:].rearrange("p a (w t) -> p t (a w)", t=SLOTS),
         )
 
-        gather_words(0, 0, HALF)
-        gather_words(0, HALF, HALF)
-        gather_words(1, 0, S)
-        gather_words(2, 0, HALF)
-        gather_words(2, HALF, HALF)
         for a in range(PASSES):
             for half in range(2):
-                for t in range(SLOTS):
-                    if (t, half) != (LATE, 1):
-                        inhibit(t, half, a)
+                gather_words(a, half)
+        for u in range(WARM):
+            nc.tensor.matmul_mx(
+                out=banks[BANKS - 1 - u][:],
+                lhsT=wi_codes[:, u, 0, :].bitcast(FP4X4),
+                lhsT_scale=picked_sc[:, 0:P],
+                rhs=tab[0][:, 0:HALF].bitcast(FP8X4),
+                rhs_scale=picked_sc[:, 0:HALF],
+                start=True,
+                stop=True,
+            )
+        tiles = [(t, half) for half in range(2) for t in range(SLOTS)]
+        for a in range(PASSES):
+            for t, half in tiles:
+                turned = (t, half) in tiles[-2:]
+                if a != 1 or not turned:
+                    inhibit(t, half, a, a == 0, a == 2 and not turned)
+                if a == 2 and turned:
+                    inhibit(t, half, 1, False, True)
 
-        we_bf = [[sbuf(f"we_bf{a}_{u}", [P, 2 * H], BF16) for u in range(2)] for a in range(2)]
-        for u in range(2):
-            round_we(0, 2 * u, 2, we_bf[0][u][:], u == 1)
-        for u in range(2):
-            quantize_we(0, 2 * u, 2, we_bf[0][u][:])
-        for t in range(SLOTS):
-            rectify_i(t, 0, sbuf(f"relu_i{t}_0", [P, HALF], F32)[:])
-        rectify_i(1, 1, stage[:, 0, :])
-        for t in range(SLOTS):
-            excite(t, 0, 0)
-        for u in range(2):
-            round_we(1, 2 * u, 2, we_bf[1][u][:], True)
-        quantize_we(1, 0, 2, we_bf[1][0][:])
+        def run(first):
+            return shared[:, first : first + 2, :].rearrange("p u c -> p (u c)")
+
+        diff[3, 1], diff[1, 0], diff[0, 0], diff[0, 1] = run(0), run(1), run(2), run(3)
+        diff[3, 0] = stage[:, 1, :]
+        for t, half in tiles:
+            if (t, half) not in diff:
+                diff[t, half] = sbuf(f"diff{t}_{half}", [P, HALF], F32, f"diff{t}_{half}")[:]
+
+        order = {tile: (0, 2, 1) for tile in tiles}
+        order[0, 0] = (0, 1, 2)
+        order[2, 1] = order[3, 1] = (2, 0, 1)
+
+        def passes(some, a):
+            for tile in some:
+                excite(tile[0], tile[1], a, order[tile][0] == a, order[tile][2] == a)
+
+        shares = (((0, 2, True), (2, 1, True), (3, 1, False)), ((0, 2, True), (2, 2, True)))
+        for a in range(2):
+            rounded = [round_we(a, *share) for share in shares[a]]
+            for share, values in zip(shares[a], rounded):
+                quantize_we(a, share[0], share[1], values)
+            if a == 0:
+                for t, half in tiles:
+                    if (t, half) == (1, 1):
+                        rectify_i(t, half, stage[:, 0, :])
+                    elif (t, half) != LATE:
+                        rectify_i(t, half, sbuf(f"relu_i{t}_{half}", [P, HALF], F32)[:])
+            passes([tile for tile in tiles if order[tile][a] == a], a)
+        rounded = [round_we(2, t, 1, True, "slot_late" if t == 0 else None) for t in range(2)]
+        quantize_we(2, 0, 1, rounded[0])
+        rounded += [round_we(2, t, 1, t == 2) for t in (2, 3)]
+        rectify_i(LATE[0], LATE[1], sbuf("relu_i_late", [P, HALF], F32, "slot_late")[:])
+        for t in (1, 2, 3):
+            quantize_we(2, t, 1, rounded[t])
+        passes([(0, 0)], 2)
+        for lo in (0, CHUNK):
+            subtract(0, 0, lo, CHUNK)
+        for lo in (0, CHUNK):
+            apply_gain(0, lo, CHUNK)
+        for tile in ((0, 1), (1, 0), (2, 0), (3, 0)):
+            for a in (2, 1):
+                passes([tile], a)
+        subtract_beside(0, 1)
+        subtract(1, 0)
+        subtract(2, 0)
+        subtract(3, 0, 0, CHUNK)
+        apply_gain(1, 0, HALF)
+        for a in order[3, 1]:
+            passes([(3, 1)], a)
+        subtract_beside(3, 1)
+        for a in (2, 0):
+            passes([LATE], a)
+        for a in (2, 1):
+            passes([(1, 1)], a)
+        passes([LATE], 1)
+        subtract(1, 1)
+        subtract(3, 0, CHUNK, CHUNK)
+        subtract(*LATE)
         for t in range(2):
-            excite(t, 0, 1)
-        we_bf2 = [sbuf(f"we_bf2_{t}", [P, H], BF16, f"slot_r{t}") for t in range(SLOTS)]
-        for t in range(SLOTS):
-            round_we(2, t, 1, we_bf2[t][:], t < 2)
-        for t in range(SLOTS):
-            quantize_we(2, t, 1, we_bf2[t][:])
-        quantize_we(1, 2, 2, we_bf[1][1][:], "slot_r0")
-        for t in range(SLOTS):
-            for a in range(2 if t < 2 else 1, PASSES):
-                excite(t, 0, a)
-
-        last = SLOTS - 1
-        flat = stage[:].rearrange("p r c -> p (r c)")
-        h_first = stage[:, 2:, :]
-        third = flat[:, 0:1024].rearrange("p (t c) -> p t c", t=SLOTS)
-        fourth = flat[:, 768:1792].rearrange("p (t c) -> p t c", t=SLOTS)
-        for t in range(SLOTS):
-            diff[t, 0] = sbuf(f"diff{t}_0", [P, HALF], F32)[:] if t < last else stage[:, 1, :]
-            subtract(t, 0)
-            if t < last:
-                apply_gain(t, 0, HALF, h_first[:, t, :], diff[t, 0])
-
-        for k, t in enumerate((0, 3)):
-            rectify_i(t, 1, sbuf(f"relu_i{t}_1", [P, HALF], F32, f"slot_r{k + 1}")[:])
-        for t in (0, 3, 2, 1):
-            diff[t, 1] = sbuf(f"diff{t}_1", [P, HALF], F32, "diff1_0" if t == 1 else None)[:]
-            if t == last:
-                for a in range(PASSES):
-                    inhibit(LATE, 1, a)
-                rectify_i(LATE, 1, sbuf("relu_i_late", [P, HALF], F32)[:])
-            for a in range(PASSES):
-                excite(t, 1, a)
-            if t in (0, 3):
-                subtract_beside(t, 1, "relu_i3_0" if t == 3 else "relu_i1_0")
-            else:
-                subtract(t, 1)
-
+            apply_gain(t, 2 * CHUNK, CHUNK)
         wo_bf = sbuf("wo_bf", [P, SLOTS * N], BF16)
         nc.scalar.activation(
             wo_bf[:].rearrange("p (c i t) -> p c t i", i=4, t=SLOTS),
@@ -298,28 +342,24 @@ def tile_list_net_drive_trials_kernel(tc, tab_words, tab_scales, offs, we, wi_wo
                 scales=wo_sc[:, first : first + width],
                 in_=wo_bf[:, 4 * first : 4 * (first + width)],
             )
+        apply_gain(2, 0, HALF)
 
+        for first in (0, CHUNK):
+            apply_gain(3, first, CHUNK)
+        for first in (0, CHUNK):
+            round_h(first, 0, CHUNK, False)
+        for t in (2, 3):
+            apply_gain(t, 2 * CHUNK, CHUNK)
+        round_h(2 * CHUNK, 0, CHUNK, False)
+        for step in range(3):
+            emit(CHUNK * step, CHUNK, "sss", product(step, CHUNK * step, CHUNK), True)
+        for t in (1, 2, 3):
+            apply_gain(t, 3 * CHUNK, CHUNK)
         for u in range(2):
-            cols = slice(256 * u, 256 * (u + 1))
-            apply_gain(last, 256 * u, 256, h_first[:, last, cols], diff[last, 0][:, cols])
-        rounded = [round_h(256 * u, 256, False, h_first[:, :, 256 * u : 256 * (u + 1)]) for u in range(2)]
-        sums0 = product(0, 0, 256, rounded[0])
-        sums1 = product(1, 256, 256, rounded[1])
-        for t in range(SLOTS):
-            apply_gain(t, 512, 256, third[:, t, :], diff[t, 1][:, 0:256])
-        rounded.append(round_h(512, 256, False, third))
-        emit(0, 256, "sss", sums0, True)
-        emit(256, 256, "sss", sums1, True)
-        sums2 = product(2, 512, 256, rounded[2])
-        for t in (1, 3, 2):
-            apply_gain(t, 768, 256, fourth[:, t, :], diff[t, 1][:, 256:512])
+            apply_gain(0, 3 * CHUNK + P * u, P)
         for u in range(2):
-            apply_gain(
-                0, 768 + 128 * u, 128, fourth[:, 0, 128 * u : 128 * (u + 1)], diff[0, 1][:, 256 + 128 * u : 384 + 128 * u]
-            )
-        emit(512, 256, "sss", sums2, True)
-        ends = [round_h(768 + 128 * u, 128, True, fourth[:, :, 128 * u : 128 * (u + 1)]) for u in range(2)]
-        sums = [product(3 + u, 768 + 128 * u, 128, ends[u]) for u in range(2)]
+            round_h(3 * CHUNK + P * u, 0, P, True)
+        sums = [product(3 + u, 3 * CHUNK + P * u, P) for u in range(2)]
         emit(768, 128, "svs", sums[0], False)
         emit(896, 128, "vsv", sums[1], False)
         for c in range(OUT_TILES):

@@ -25,7 +25,6 @@ BANKS = 8
 CHUNK = 256
 QUADRANTS = (0, 2, 1, 3)
 WARM = 3
-TAB2_CUT = 512
 LATE = (2, 1)
 
 
@@ -61,7 +60,8 @@ def tile_list_net_drive_trials_kernel(tc, tab_words, tab_scales, offs, we, wi_wo
         flat = stage[:].rearrange("p u c -> p (u c)")
         third = flat[:, 0:1024].rearrange("p (t c) -> p t c", t=SLOTS)
         fourth = flat[:, 768:1792].rearrange("p (t c) -> p t c", t=SLOTS)
-        shared = sbuf("shared", [P, 5, CHUNK], F32)
+        shared = sbuf("shared", [P, 11 * P], F32)
+        first_rest = sbuf("first_rest", [P, CHUNK], F32)
         h_bf = {first: sbuf(f"h_bf{first}", [P, SLOTS * CHUNK], BF16)[:] for first in (0, CHUNK, 2 * CHUNK)}
         for first in (3 * CHUNK, 3 * CHUNK + P):
             h_bf[first] = sbuf(f"h_bf{first}", [P, SLOTS * P], BF16)[:]
@@ -135,8 +135,10 @@ def tile_list_net_drive_trials_kernel(tc, tab_words, tab_scales, offs, we, wi_wo
             nc.scalar.activation(dst, bank[t, half][:], ACT.Relu)
 
         def differences(t, half, cols):
+            if (t, half) == (0, 0):
+                return first_rest[:] if cols.start else shared[:, 6 * P : 8 * P]
             if (t, half) == (3, 0) and cols.start:
-                return shared[:, 2, :]
+                return shared[:, 5 * P : 7 * P]
             return diff[t, half][:, cols]
 
         def subtract(t, half, lo=0, width=HALF):
@@ -214,21 +216,19 @@ def tile_list_net_drive_trials_kernel(tc, tab_words, tab_scales, offs, we, wi_wo
             )
         load_tab(0)
         load_tab(1)
-        load_tab(2, 0, TAB2_CUT)
 
         nc.vector.tensor_copy(picked_sc[:], tab_sc[:].bitcast(U8).indirect(picks(0, S)))
         for q in QUADRANTS:
             nc.sync.dma_start(
                 v_sc_early[32 * q : 32 * q + 4, :, :].bitcast(I32), picked_sc[32 * q : 32 * q + 32 : 4, :].bitcast(I32)
             )
-        load_tab(2, TAB2_CUT, T)
-        load_we(0)
+        load_tab(2)
         for q in QUADRANTS:
             nc.sync.dma_start(
                 v_sc_last[32 * q : 32 * q + 4, :].bitcast(I32), picked_sc[32 * q + 6 : 32 * q + 32 : 8, :].bitcast(I32)
             )
-        load_we(1)
-        load_we(2)
+        for a in range(PASSES):
+            load_we(a)
         load_gain(0)
         load_gain(1)
         for t in range(SLOTS):
@@ -269,13 +269,11 @@ def tile_list_net_drive_trials_kernel(tc, tab_words, tab_scales, offs, we, wi_wo
                 if a == 2 and turned:
                     inhibit(t, half, 1, False, True)
 
-        def run(first):
-            return shared[:, first : first + 2, :].rearrange("p u c -> p (u c)")
-
-        diff[3, 1], diff[1, 0], diff[0, 0], diff[0, 1] = run(0), run(1), run(2), run(3)
+        for tile, first in (((3, 1), 0), ((1, 0), 3 * P), ((0, 1), 7 * P)):
+            diff[tile] = shared[:, first : first + HALF]
         diff[3, 0] = stage[:, 1, :]
         for t, half in tiles:
-            if (t, half) not in diff:
+            if (t, half) not in diff and (t, half) != (0, 0):
                 diff[t, half] = sbuf(f"diff{t}_{half}", [P, HALF], F32, f"diff{t}_{half}")[:]
 
         order = {tile: (0, 2, 1) for tile in tiles}
@@ -295,15 +293,16 @@ def tile_list_net_drive_trials_kernel(tc, tab_words, tab_scales, offs, we, wi_wo
                 for t, half in tiles:
                     if (t, half) == (1, 1):
                         rectify_i(t, half, stage[:, 0, :])
-                    elif (t, half) != LATE:
+                    elif (t, half) not in tiles[-2:]:
                         rectify_i(t, half, sbuf(f"relu_i{t}_{half}", [P, HALF], F32)[:])
             passes([tile for tile in tiles if order[tile][a] == a], a)
-        rounded = [round_we(2, t, 1, True, "slot_late" if t == 0 else None) for t in range(2)]
+        rounded = [round_we(2, t, 1, True, f"slot_late{t}") for t in range(2)]
         quantize_we(2, 0, 1, rounded[0])
         rounded += [round_we(2, t, 1, t == 2) for t in (2, 3)]
-        rectify_i(LATE[0], LATE[1], sbuf("relu_i_late", [P, HALF], F32, "slot_late")[:])
         for t in (1, 2, 3):
             quantize_we(2, t, 1, rounded[t])
+        for u, t in enumerate((3, 2)):
+            rectify_i(t, 1, sbuf(f"relu_i{t}_1", [P, HALF], F32, f"slot_late{u}")[:])
         passes([(0, 0)], 2)
         for lo in (0, CHUNK):
             subtract(0, 0, lo, CHUNK)
@@ -316,7 +315,8 @@ def tile_list_net_drive_trials_kernel(tc, tab_words, tab_scales, offs, we, wi_wo
         subtract(1, 0)
         subtract(2, 0)
         subtract(3, 0, 0, CHUNK)
-        apply_gain(1, 0, HALF)
+        for lo in (0, CHUNK):
+            apply_gain(1, lo, CHUNK)
         for a in order[3, 1]:
             passes([(3, 1)], a)
         subtract_beside(3, 1)

@@ -24,7 +24,6 @@ OUT_TILES = N // P
 BANKS = 8
 CHUNK = 256
 QUADRANTS = (0, 2, 1, 3)
-WARM = 3
 LATE = (2, 1)
 
 
@@ -47,7 +46,6 @@ def tile_list_net_drive_trials_kernel(tc, tab_words, tab_scales, offs, we, wi_wo
         wi_sc_raw = sbuf("wi_sc_raw", [P, PASSES, H // 4], I32)
         wi_sc = sbuf("wi_sc", [P, SLOTS, PASSES, P], U8)
         wo_raw = sbuf("wo_raw", [P, SLOTS, N], F32)
-        wo_codes = sbuf("wo_codes", [P, N], U32)
         wo_sc = sbuf("wo_sc", [P, N], U8)
         bias = sbuf("bias", [P, OUT_TILES], F32)
         result = sbuf("result", [P, OUT_TILES, S], F32)
@@ -56,10 +54,8 @@ def tile_list_net_drive_trials_kernel(tc, tab_words, tab_scales, offs, we, wi_wo
         gain = [sbuf(f"gain{t}", [P, T], F32) for t in range(SLOTS)]
         banks = [psum.tile([P, HALF], F32, name=f"bank{b}") for b in range(BANKS)]
         bank = {(t, half): banks[SLOTS * half + t] for t in range(SLOTS) for half in range(2)}
-        stage = sbuf("stage", [P, SLOTS + 2, HALF], F32)
-        flat = stage[:].rearrange("p u c -> p (u c)")
-        third = flat[:, 0:1024].rearrange("p (t c) -> p t c", t=SLOTS)
-        fourth = flat[:, 768:1792].rearrange("p (t c) -> p t c", t=SLOTS)
+        stage = sbuf("stage", [P, SLOTS + 1, HALF], F32)
+        third = sbuf("third", [P, SLOTS, HALF], F32)
         shared = sbuf("shared", [P, 11 * P], F32)
         first_rest = sbuf("first_rest", [P, CHUNK], F32)
         h_bf = {first: sbuf(f"h_bf{first}", [P, SLOTS * CHUNK], BF16)[:] for first in (0, CHUNK, 2 * CHUNK)}
@@ -155,8 +151,8 @@ def tile_list_net_drive_trials_kernel(tc, tab_words, tab_scales, offs, we, wi_wo
         def h_cols(first, width):
             chunk, lo = divmod(first, CHUNK)
             if chunk < 2:
-                return stage[:, 2:, first : first + width]
-            return (third if chunk == 2 else fourth)[:, :, lo : lo + width]
+                return stage[:, :SLOTS, first : first + width]
+            return (third[:] if chunk == 2 else stage[:, 1:, :])[:, :, lo : lo + width]
 
         def apply_gain(t, first, width):
             half, lo = divmod(first, HALF)
@@ -165,9 +161,10 @@ def tile_list_net_drive_trials_kernel(tc, tab_words, tab_scales, offs, we, wi_wo
                 h_cols(first, width)[:, t, :], gain[t][:].indirect(picks(first, width)), differences(t, half, cols), ALU.mult
             )
 
-        def round_h(first, lo, width, on_vector):
-            values = h_cols(first + lo, width)
+        def round_h(first, lo, width, on_vector, t=0, count=SLOTS):
+            values = h_cols(first + lo, width)[:, t : t + count, :]
             h_dst = h_bf[first][:, SLOTS * lo : SLOTS * (lo + width)].rearrange("p (c i t) -> p c t i", i=4, t=SLOTS)
+            h_dst = h_dst[:, :, t : t + count, :]
             h_src = values.rearrange("p t (c i) -> p c t i", i=4)
             if on_vector:
                 nc.vector.tensor_copy(h_dst, h_src)
@@ -223,12 +220,13 @@ def tile_list_net_drive_trials_kernel(tc, tab_words, tab_scales, offs, we, wi_wo
                 v_sc_early[32 * q : 32 * q + 4, :, :].bitcast(I32), picked_sc[32 * q : 32 * q + 32 : 4, :].bitcast(I32)
             )
         load_tab(2)
+        load_we(0)
         for q in QUADRANTS:
             nc.sync.dma_start(
                 v_sc_last[32 * q : 32 * q + 4, :].bitcast(I32), picked_sc[32 * q + 6 : 32 * q + 32 : 8, :].bitcast(I32)
             )
-        for a in range(PASSES):
-            load_we(a)
+        load_we(1)
+        load_we(2)
         load_gain(0)
         load_gain(1)
         for t in range(SLOTS):
@@ -250,16 +248,6 @@ def tile_list_net_drive_trials_kernel(tc, tab_words, tab_scales, offs, we, wi_wo
         for a in range(PASSES):
             for half in range(2):
                 gather_words(a, half)
-        for u in range(WARM):
-            nc.tensor.matmul_mx(
-                out=banks[BANKS - 1 - u][:],
-                lhsT=wi_codes[:, u, 0, :].bitcast(FP4X4),
-                lhsT_scale=picked_sc[:, 0:P],
-                rhs=tab[0][:, 0:HALF].bitcast(FP8X4),
-                rhs_scale=picked_sc[:, 0:HALF],
-                start=True,
-                stop=True,
-            )
         tiles = [(t, half) for half in range(2) for t in range(SLOTS)]
         for a in range(PASSES):
             for t, half in tiles:
@@ -271,14 +259,13 @@ def tile_list_net_drive_trials_kernel(tc, tab_words, tab_scales, offs, we, wi_wo
 
         for tile, first in (((3, 1), 0), ((1, 0), 3 * P), ((0, 1), 7 * P)):
             diff[tile] = shared[:, first : first + HALF]
-        diff[3, 0] = stage[:, 1, :]
         for t, half in tiles:
             if (t, half) not in diff and (t, half) != (0, 0):
                 diff[t, half] = sbuf(f"diff{t}_{half}", [P, HALF], F32, f"diff{t}_{half}")[:]
 
         order = {tile: (0, 2, 1) for tile in tiles}
         order[0, 0] = (0, 1, 2)
-        order[2, 1] = order[3, 1] = (2, 0, 1)
+        order[1, 1] = order[2, 1] = order[3, 1] = (2, 0, 1)
 
         def passes(some, a):
             for tile in some:
@@ -292,7 +279,7 @@ def tile_list_net_drive_trials_kernel(tc, tab_words, tab_scales, offs, we, wi_wo
             if a == 0:
                 for t, half in tiles:
                     if (t, half) == (1, 1):
-                        rectify_i(t, half, stage[:, 0, :])
+                        rectify_i(t, half, third[:, 0, :])
                     elif (t, half) not in tiles[-2:]:
                         rectify_i(t, half, sbuf(f"relu_i{t}_{half}", [P, HALF], F32)[:])
             passes([tile for tile in tiles if order[tile][a] == a], a)
@@ -322,14 +309,19 @@ def tile_list_net_drive_trials_kernel(tc, tab_words, tab_scales, offs, we, wi_wo
         subtract_beside(3, 1)
         for a in (2, 0):
             passes([LATE], a)
-        for a in (2, 1):
+        for a in order[1, 1]:
             passes([(1, 1)], a)
         passes([LATE], 1)
         subtract(1, 1)
         subtract(3, 0, CHUNK, CHUNK)
         subtract(*LATE)
-        for t in range(2):
-            apply_gain(t, 2 * CHUNK, CHUNK)
+        for first in (0, CHUNK):
+            round_h(first, 0, CHUNK, False, 0, 2)
+        for t, chunk in ((0, 2), (1, 2), (0, 3)):
+            apply_gain(t, CHUNK * chunk, CHUNK)
+        apply_gain(2, 0, HALF)
+        apply_gain(2, 2 * CHUNK, CHUNK)
+        wo_codes = sbuf("wo_codes", [P, N], U32, "diff2_0")
         wo_bf = sbuf("wo_bf", [P, SLOTS * N], BF16)
         nc.scalar.activation(
             wo_bf[:].rearrange("p (c i t) -> p c t i", i=4, t=SLOTS),
@@ -342,21 +334,21 @@ def tile_list_net_drive_trials_kernel(tc, tab_words, tab_scales, offs, we, wi_wo
                 scales=wo_sc[:, first : first + width],
                 in_=wo_bf[:, 4 * first : 4 * (first + width)],
             )
-        apply_gain(2, 0, HALF)
+        round_h(2 * CHUNK, 0, CHUNK, False, 0, 2)
 
-        for first in (0, CHUNK):
-            apply_gain(3, first, CHUNK)
-        for first in (0, CHUNK):
-            round_h(first, 0, CHUNK, False)
-        for t in (2, 3):
-            apply_gain(t, 2 * CHUNK, CHUNK)
-        round_h(2 * CHUNK, 0, CHUNK, False)
-        for step in range(3):
-            emit(CHUNK * step, CHUNK, "sss", product(step, CHUNK * step, CHUNK), True)
-        for t in (1, 2, 3):
-            apply_gain(t, 3 * CHUNK, CHUNK)
+        for chunk in range(4):
+            apply_gain(3, CHUNK * chunk, CHUNK)
+        for chunk in range(3):
+            round_h(CHUNK * chunk, 0, CHUNK, False, 2, 2)
+        sums0 = product(0, 0, CHUNK)
+        sums1 = product(1, CHUNK, CHUNK)
+        emit(0, CHUNK, "sss", sums0, True)
+        sums2 = product(2, 2 * CHUNK, CHUNK)
+        apply_gain(1, 3 * CHUNK, CHUNK)
         for u in range(2):
-            apply_gain(0, 3 * CHUNK + P * u, P)
+            apply_gain(2, 3 * CHUNK + P * u, P)
+        emit(CHUNK, CHUNK, "sss", sums1, True)
+        emit(2 * CHUNK, CHUNK, "sss", sums2, True)
         for u in range(2):
             round_h(3 * CHUNK + P * u, 0, P, True)
         sums = [product(3 + u, 3 * CHUNK + P * u, P) for u in range(2)]

from contextlib import ExitStack

import concourse.mybir as mybir

K, T, S, H, N = 1536, 2048, 1024, 512, 384
FLOPS = 2 * S * (2 * K * H + H * N)

F32 = mybir.dt.float32
BF16 = mybir.dt.bfloat16
I32 = mybir.dt.int32
U32 = mybir.dt.uint32
U16 = mybir.dt.uint16
U8 = mybir.dt.uint8
FP8X4 = mybir.dt.float8_e4m3fn_x4
FP4X4 = mybir.dt.float4_e2m1fn_x4
ALU = mybir.AluOpType
ACT = mybir.ActivationFunctionType

P = 128
PASSES = K // 512
SLOTS = 4
HALF = 512
OUT_TILES = N // P
BANKS = 8
CHUNK = 256
QUADRANTS = (0, 2, 1, 3)
LATE = (2, 1)


def tile_list_net_drive_trials_kernel(tc, tab_words, tab_scales, offs, we, wi_words, wi_scales, gT, wo, bo, out):
    nc = tc.nc
    with ExitStack() as ctx:
        keep = ctx.enter_context(tc.tile_pool(name="keep", bufs=1))
        psum = ctx.enter_context(tc.psum_pool(name="psum", bufs=1))

        def sbuf(name, shape, dtype, slot=None):
            return keep.tile(shape, dtype, name=name, tag=slot or name, align_bytes=64)

        offsets = keep.tile([P, S // 16], U16, name="offsets")
        tab_sc = sbuf("tab_sc", [P, T // 4], I32, "slot_sc")
        picked_sc = sbuf("picked_sc", [P, S], U8)
        v_sc_early = sbuf("v_sc_early", [P, 2, S], U8)
        v_sc_last = sbuf("v_sc_last", [P, S], U8)
        v_sc = [v_sc_early[:, 0, :], v_sc_early[:, 1, :], v_sc_last[:]]
        wi_raw = sbuf("wi_raw", [P, PASSES, 2 * H // 4], I32)
        wi_sc_raw = sbuf("wi_sc_raw", [P, PASSES, H // 4], I32)
        wi_sc = sbuf("wi_sc", [P, SLOTS, PASSES, P], U8)
        wo_raw = sbuf("wo_raw", [P, SLOTS, N], F32)
        wo_sc = sbuf("wo_sc", [P, N], U8)
        bias = sbuf("bias", [P, OUT_TILES], F32)
        result = sbuf("result", [P, OUT_TILES, S], F32)
        tab = [sbuf(f"tab{a}", [P, T], I32) for a in range(PASSES)]
        we_raw = [sbuf(f"we_raw{a}", [P, SLOTS, H], F32) for a in range(PASSES)]
        gain = [sbuf(f"gain{t}", [P, T], F32) for t in range(SLOTS)]
        banks = [psum.tile([P, HALF], F32, name=f"bank{b}") for b in range(BANKS)]
        bank = {(t, half): banks[SLOTS * half + t] for t in range(SLOTS) for half in range(2)}
        stage = sbuf("stage", [P, SLOTS + 1, HALF], F32)
        third = sbuf("third", [P, SLOTS, HALF], F32)
        shared = sbuf("shared", [P, 11 * P], F32)
        first_rest = sbuf("first_rest", [P, CHUNK], F32)
        h_bf = {first: sbuf(f"h_bf{first}", [P, SLOTS * CHUNK], BF16)[:] for first in (0, CHUNK, 2 * CHUNK)}
        for first in (3 * CHUNK, 3 * CHUNK + P):
            h_bf[first] = sbuf(f"h_bf{first}", [P, SLOTS * P], BF16)[:]
        v_words, we_codes, we_sc, relu_i, diff = {}, {}, {}, {}, {}

        gain_rows = gT.rearrange("(w t b) c -> t w b c", t=SLOTS, b=4)
        wo_rows = wo.rearrange("(w t b) n -> t w b n", t=SLOTS, b=4)
        out_rows = out.rearrange("(c p) j -> p c j", p=P)

        def picks(first, width):
            return offsets[:, first // 16 : (first + width) // 16]

        def load_tab(a, first=0, last=T):
            words = tab_words[a].rearrange("p t i -> p (t i)").bitcast(I32)
            nc.sync.dma_start(tab[a][:, first:last], words[:, first:last])

        def load_we(a):
            nc.sync.dma_start(we_raw[a][:], we[512 * a : 512 * (a + 1), :].rearrange("(p j) r -> p j r", j=4))

        def load_gain(t):
            nc.sync.dma_start(gain[t][:], gain_rows[t])

        def gather_words(a, half, slot=None):
            picked = sbuf(f"v_words{a}_{half}", [P, HALF], U32, slot)
            nc.vector.tensor_copy(picked[:], tab[a][:].bitcast(U32).indirect(picks(HALF * half, HALF)))
            v_words[a, half] = picked[:]

        def round_we(a, t, count, on_vector, slot=None):
            rounded = sbuf(f"we_bf{a}_{t}", [P, count * H], BF16, slot)
            dst = rounded[:].rearrange("p (t w b j) -> p t w j b", t=count, b=4, j=4)
            src = we_raw[a][:].rearrange("p j (w t b) -> p t w j b", t=SLOTS, b=4)[:, t : t + count]
            if on_vector:
                nc.vector.tensor_copy(dst, src)
            else:
                for u in range(count):
                    nc.scalar.activation(dst[:, u], src[:, u], ACT.Copy)
            return rounded[:]

        def quantize_we(a, t, count, rounded):
            codes = sbuf(f"we_codes{a}_{t}", [P, P * count], U32)
            scales = sbuf(f"we_sc{a}_{t}", [P, P * count], U8)
            nc.vector.quantize_mx(out=codes[:].bitcast(FP8X4), scales=scales[:], in_=rounded)
            for u in range(count):
                we_codes[a, t + u] = codes[:, P * u : P * (u + 1)]
                we_sc[a, t + u] = scales[:, P * u : P * (u + 1)]

        def excite(t, half, a, start, stop):
            nc.tensor.matmul_mx(
                out=bank[t, half][:],
                lhsT=we_codes[a, t].bitcast(FP8X4),
                lhsT_scale=we_sc[a, t],
                rhs=v_words[a, half].bitcast(FP8X4),
                rhs_scale=v_sc[a][:, HALF * half : HALF * (half + 1)],
                start=start,
                stop=stop,
            )

        def inhibit(t, half, a, start, stop):
            nc.tensor.matmul_mx(
                out=bank[t, half][:],
                lhsT=wi_codes[:, t, a, :].bitcast(FP4X4),
                lhsT_scale=wi_sc[:, t, a, :],
                rhs=v_words[a, half].bitcast(FP8X4),
                rhs_scale=v_sc[a][:, HALF * half : HALF * (half + 1)],
                start=start,
                stop=stop,
            )

        def rectify_i(t, half, dst):
            relu_i[t, half] = dst
            nc.scalar.activation(dst, bank[t, half][:], ACT.Relu)

        def differences(t, half, cols):
            if (t, half) == (0, 0):
                return first_rest[:] if cols.start else shared[:, 6 * P : 8 * P]
            if (t, half) == (3, 0) and cols.start:
                return shared[:, 5 * P : 7 * P]
            return diff[t, half][:, cols]

        def subtract(t, half, lo=0, width=HALF):
            cols = slice(lo, lo + width)
            nc.vector.scalar_tensor_tensor(
                differences(t, half, cols), bank[t, half][:, cols], 0.0, relu_i[t, half][:, cols], ALU.max, ALU.subtract
            )

        def subtract_beside(t, half):
            relu_e = sbuf(f"relu_e{t}_{half}", [P, HALF], F32)
            nc.scalar.activation(relu_e[:], bank[t, half][:], ACT.Relu)
            nc.gpsimd.tensor_tensor(diff[t, half], relu_e[:], relu_i[t, half], ALU.subtract)

        def h_cols(first, width):
            chunk, lo = divmod(first, CHUNK)
            if chunk < 2:
                return stage[:, :SLOTS, first : first + width]
            return (third[:] if chunk == 2 else stage[:, 1:, :])[:, :, lo : lo + width]

        def apply_gain(t, first, width):
            half, lo = divmod(first, HALF)
            cols = slice(lo, lo + width)
            nc.vector.tensor_tensor(
                h_cols(first, width)[:, t, :], gain[t][:].indirect(picks(first, width)), differences(t, half, cols), ALU.mult
            )

        def round_h(first, lo, width, on_vector, t=0, count=SLOTS):
            values = h_cols(first + lo, width)[:, t : t + count, :]
            h_dst = h_bf[first][:, SLOTS * lo : SLOTS * (lo + width)].rearrange("p (c i t) -> p c t i", i=4, t=SLOTS)
            h_dst = h_dst[:, :, t : t + count, :]
            h_src = values.rearrange("p t (c i) -> p c t i", i=4)
            if on_vector:
                nc.vector.tensor_copy(h_dst, h_src)
            else:
                nc.scalar.activation(h_dst, h_src, ACT.Copy)

        def product(step, first, width):
            h_codes = sbuf(f"h_codes{first}", [P, width], U32)
            h_sc = sbuf(f"h_sc{first}", [P, width], U8)
            nc.vector.quantize_mx(out=h_codes[:].bitcast(FP8X4), scales=h_sc[:], in_=h_bf[first])
            sums = [banks[(OUT_TILES * step + c) % BANKS][:, :width] for c in range(OUT_TILES)]
            for c in range(OUT_TILES):
                nc.tensor.matmul_mx(
                    out=sums[c],
                    lhsT=wo_codes[:, P * c : P * (c + 1)].bitcast(FP8X4),
                    lhsT_scale=wo_sc[:, P * c : P * (c + 1)],
                    rhs=h_codes[:].bitcast(FP8X4),
                    rhs_scale=h_sc[:],
                    start=True,
                    stop=True,
                )
            return sums

        def emit(first, width, empty_on, sums, by_tile):
            cols = slice(first, first + width)
            for c in range(OUT_TILES):
                if empty_on[c] == "s":
                    nc.scalar.activation(result[:, c, cols], sums[c], ACT.Identity, bias=bias[:, c : c + 1])
                else:
                    nc.vector.tensor_scalar(result[:, c, cols], sums[c], bias[:, c : c + 1], None, ALU.add)
                if by_tile:
                    nc.sync.dma_start(out_rows[:, c, cols], result[:, c, cols])

        nc.vector.memset(tab_sc[:], 0)
        nc.vector.memset(v_sc_early[:].rearrange("p a s -> p (a s)").bitcast(I32), 0)
        nc.vector.memset(v_sc_last[:].bitcast(I32), 0)
        nc.vector.memset(wi_sc_raw[:], 0)
        nc.sync.dma_start(offsets[:], offs)
        nc.sync.dma_start(wi_raw[:], wi_words.bitcast(I32).rearrange("a p c -> p a c"))
        nc.sync.dma_start(tab_sc[0:P:4, :], tab_scales[0:2].bitcast(I32).rearrange("a j c -> j a c"))
        nc.sync.dma_start(tab_sc[6:P:8, :], tab_scales[2].bitcast(I32))
        for r in range(4):
            nc.scalar.dma_start(
                wi_sc_raw[r:P:32, :, :],
                wi_scales.bitcast(I32).rearrange("a (q r) c -> r q a c", r=4)[r],
            )
        load_tab(0)
        load_tab(1)

        nc.vector.tensor_copy(picked_sc[:], tab_sc[:].bitcast(U8).indirect(picks(0, S)))
        for q in QUADRANTS:
            nc.sync.dma_start(
                v_sc_early[32 * q : 32 * q + 4, :, :].bitcast(I32), picked_sc[32 * q : 32 * q + 32 : 4, :].bitcast(I32)
            )
        load_tab(2)
        load_we(0)
        for q in QUADRANTS:
            nc.sync.dma_start(
                v_sc_last[32 * q : 32 * q + 4, :].bitcast(I32), picked_sc[32 * q + 6 : 32 * q + 32 : 8, :].bitcast(I32)
            )
        load_we(1)
        load_we(2)
        load_gain(0)
        load_gain(1)
        for t in range(SLOTS):
            nc.sync.dma_start(wo_raw[:, t, :], wo_rows[t])
        load_gain(2)
        load_gain(3)
        with nc.allow_non_contiguous_dma(reason="one bias value for each partition and output tile"):
            nc.sync.dma_start(bias[:], bo.rearrange("(c p) -> p c", p=P))
        wi_codes = sbuf("wi_codes", [P, SLOTS, PASSES, 2 * P], U8, "slot_sc")
        nc.vector.tensor_copy(
            wi_codes[:].rearrange("p t a c -> p t (a c)").bitcast(I32).rearrange("p t (u e) -> p t u e", e=2),
            wi_raw[:].rearrange("p a (w t e) -> p t (a w) e", t=SLOTS, e=2),
        )
        nc.vector.tensor_copy(
            wi_sc[:].rearrange("p t a c -> p t (a c)").bitcast(I32),
            wi_sc_raw[:].rearrange("p a (w t) -> p t (a w)", t=SLOTS),
        )

        for a in range(PASSES):
            for half in range(2):
                gather_words(a, half)
        tiles = [(t, half) for half in range(2) for t in range(SLOTS)]
        for a in range(PASSES):
            for t, half in tiles:
                turned = (t, half) in tiles[-2:]
                if a != 1 or not turned:
                    inhibit(t, half, a, a == 0, a == 2 and not turned)
                if a == 2 and turned:
                    inhibit(t, half, 1, False, True)

        for tile, first in (((3, 1), 0), ((1, 0), 3 * P), ((0, 1), 7 * P)):
            diff[tile] = shared[:, first : first + HALF]
        for t, half in tiles:
            if (t, half) not in diff and (t, half) != (0, 0):
                diff[t, half] = sbuf(f"diff{t}_{half}", [P, HALF], F32, f"diff{t}_{half}")[:]

        order = {tile: (0, 2, 1) for tile in tiles}
        order[0, 0] = (0, 1, 2)
        order[1, 1] = order[2, 1] = order[3, 1] = (2, 0, 1)

        def passes(some, a):
            for tile in some:
                excite(tile[0], tile[1], a, order[tile][0] == a, order[tile][2] == a)

        shares = (((0, 2, True), (2, 1, True), (3, 1, False)), ((0, 2, True), (2, 2, True)))
        for a in range(2):
            rounded = [round_we(a, *share) for share in shares[a]]
            for share, values in zip(shares[a], rounded):
                quantize_we(a, share[0], share[1], values)
            if a == 0:
                for t, half in tiles:
                    if (t, half) == (1, 1):
                        rectify_i(t, half, third[:, 0, :])
                    elif (t, half) not in tiles[-2:]:
                        rectify_i(t, half, sbuf(f"relu_i{t}_{half}", [P, HALF], F32)[:])
            passes([tile for tile in tiles if order[tile][a] == a], a)
        rounded = [round_we(2, t, 1, True, f"slot_late{t}") for t in range(2)]
        quantize_we(2, 0, 1, rounded[0])
        rounded += [round_we(2, t, 1, t == 2) for t in (2, 3)]
        for t in (1, 2, 3):
            quantize_we(2, t, 1, rounded[t])
        for u, t in enumerate((3, 2)):
            rectify_i(t, 1, sbuf(f"relu_i{t}_1", [P, HALF], F32, f"slot_late{u}")[:])
        passes([(0, 0)], 2)
        for lo in (0, CHUNK):
            subtract(0, 0, lo, CHUNK)
        for lo in (0, CHUNK):
            apply_gain(0, lo, CHUNK)
        for tile in ((0, 1), (1, 0), (2, 0), (3, 0)):
            for a in (2, 1):
                passes([tile], a)
        subtract_beside(0, 1)
        subtract(1, 0)
        subtract(2, 0)
        subtract(3, 0, 0, CHUNK)
        for lo in (0, CHUNK):
            apply_gain(1, lo, CHUNK)
        for a in order[3, 1]:
            passes([(3, 1)], a)
        subtract_beside(3, 1)
        for a in (2, 0):
            passes([LATE], a)
        for a in order[1, 1]:
            passes([(1, 1)], a)
        passes([LATE], 1)
        subtract(1, 1)
        subtract(3, 0, CHUNK, CHUNK)
        subtract(*LATE)
        for first in (0, CHUNK):
            round_h(first, 0, CHUNK, False, 0, 2)
        for t, chunk in ((0, 2), (1, 2), (0, 3)):
            apply_gain(t, CHUNK * chunk, CHUNK)
        apply_gain(2, 0, HALF)
        apply_gain(2, 2 * CHUNK, CHUNK)
        wo_codes = sbuf("wo_codes", [P, N], U32, "diff2_0")
        wo_bf = sbuf("wo_bf", [P, SLOTS * N], BF16)
        nc.scalar.activation(
            wo_bf[:].rearrange("p (c i t) -> p c t i", i=4, t=SLOTS),
            wo_raw[:].rearrange("p t (c i) -> p c t i", i=4),
            ACT.Copy,
        )
        for first, width in ((0, 256), (256, 128)):
            nc.vector.quantize_mx(
                out=wo_codes[:, first : first + width].bitcast(FP8X4),
                scales=wo_sc[:, first : first + width],
                in_=wo_bf[:, 4 * first : 4 * (first + width)],
            )
        round_h(2 * CHUNK, 0, CHUNK, False, 0, 2)

        for chunk in range(4):
            apply_gain(3, CHUNK * chunk, CHUNK)
        for chunk in range(3):
            round_h(CHUNK * chunk, 0, CHUNK, False, 2, 2)
        sums0 = product(0, 0, CHUNK)
        sums1 = product(1, CHUNK, CHUNK)
        emit(0, CHUNK, "sss", sums0, True)
        sums2 = product(2, 2 * CHUNK, CHUNK)
        apply_gain(1, 3 * CHUNK, CHUNK)
        for u in range(2):
            apply_gain(2, 3 * CHUNK + P * u, P)
        emit(CHUNK, CHUNK, "sss", sums1, True)
        emit(2 * CHUNK, CHUNK, "sss", sums2, True)
        for u in range(2):
            round_h(3 * CHUNK + P * u, 0, P, True)
        sums = [product(3 + u, 3 * CHUNK + P * u, P) for u in range(2)]
        emit(768, 128, "svs", sums[0], False)
        emit(896, 128, "vsv", sums[1], False)
        for c in range(OUT_TILES):
            nc.sync.dma_start(out_rows[:, c, 768:S], result[:, c, 768:S])
